import numpy as np
import ml_dtypes


def mxq(x, axis, fmt="e4m3"):
    dtype, down = {"e4m3": (ml_dtypes.float8_e4m3fn, 7), "e5m2": (ml_dtypes.float8_e5m2, 14)}[fmt]
    v = np.moveaxis(np.asarray(x, np.float32).astype(ml_dtypes.bfloat16).astype(np.float64), axis, -1)
    blocks = v.reshape(v.shape[:-1] + (-1, 32))
    amax = np.abs(blocks).max(-1, keepdims=True)
    byte = np.maximum(np.where(amax > 0, np.frexp(amax)[1] - 1 + 127, 0) - down, 1)
    scale = np.exp2(byte - 127.0)
    codes = (blocks / scale).astype(np.float32).astype(dtype).astype(np.float64)
    return np.moveaxis((codes * scale).reshape(v.shape), -1, axis)


WIDE = False


def mx_kscale(k):
    if not WIDE:
        return np.ones(k)
    levels = np.array([10, -10, 5, -5, 0])
    if k % 512:
        return np.exp2(np.random.permutation(np.resize(levels, k // 32))).repeat(32)
    a = np.empty((k // 512, 16))
    for p in range(k // 512):
        a[p, :8] = np.random.permutation(np.resize(levels, 8))
        for g in range(8):
            far = levels[np.abs(levels - a[p, g]) >= 10]
            a[p, g + 8] = far[np.random.randint(len(far))]
    return np.exp2(a.ravel()).repeat(32)


def f64(x):
    return np.asarray(x).astype(np.float64)


def striped(idx):
    return np.tile(idx.reshape(-1, 16).T, (8, 1)).astype(np.uint16)


def unstriped(offs):
    return offs[:16].T.reshape(-1).astype(np.int64)


def pack_weight(w):
    k, n = w.shape
    w = f64(np.asarray(w, np.float32).astype(ml_dtypes.bfloat16)).reshape(k // 32, 32, n)
    amax = np.abs(w).max(1)
    byte = np.clip(np.where(amax > 0, np.frexp(amax)[1] - 1 + 127 - 7, 1), 1, 254)
    scaled = (w * np.exp2(127.0 - byte)[:, None, :]).reshape(k, n).astype(np.float32)
    words = np.ascontiguousarray(scaled.reshape(k // 512, 128, 4, n).transpose(0, 1, 3, 2)).astype(ml_dtypes.float8_e4m3fn).view(np.uint8)
    return words, np.ascontiguousarray(byte.astype(np.uint8).reshape(k // 512, 16, n))


def unpack_weight(words, scales):
    g, p, n, _ = words.shape
    vals = np.ascontiguousarray(words).view(ml_dtypes.float8_e4m3fn).astype(np.float64) * np.repeat(np.exp2(scales.astype(np.float64) - 127.0), 8, axis=1)[..., None]
    return vals.transpose(0, 1, 3, 2).reshape(g * 512, n)

def planes(y):
    n, m = y.shape
    v = y.astype(np.float32).astype(ml_dtypes.bfloat16).astype(np.float64).reshape(n // 32, 32, m)
    top = np.abs(v).max(1)
    byte = np.clip(np.where(top > 0, np.frexp(top)[1] - 1 + 127 - 7, 1), 1, 254)
    codes = (v * np.exp2(127.0 - byte)[:, None, :]).reshape(n, m).astype(np.float32).astype(ml_dtypes.float8_e4m3fn).view(np.uint8)
    words = codes.reshape(n // 512, 128, 4, m).transpose(0, 1, 3, 2)
    return np.ascontiguousarray(words), np.ascontiguousarray(byte.astype(np.uint8).reshape(n // 512, 16, m))


K, T, S, N, U = 512, 1024, 512, 512, 1024


def setup_inputs():
    n = np.random.standard_normal
    s = mx_kscale(K)[:, None]
    packed_xT = pack_weight(n((K, T)) * s)
    return {
        "x_words": packed_xT[0],
        "x_scales": packed_xT[1],
        "mem": n((N, U)).astype(np.float32),
        "w1": (n((K, N)) / np.sqrt(K) / s).astype(np.float32),
        "offs": striped(np.random.permutation(T)[:S]),
        "slot": striped(np.random.permutation(U)[:S]),
    }


def reference(x_words, x_scales, mem, w1, offs, slot):
    xq = unpack_weight(x_words, x_scales)[:, unstriped(offs)]
    y = mxq(f64(w1), 0, "e4m3").T @ xq
    out = f64(mem).copy()
    out[:, unstriped(slot)] = y
    return (out,) + planes(out)

@@ -1,0 +1,149 @@
+from contextlib import ExitStack
+
+import concourse.mybir as mybir
+
+K, T, S, N, U = 512, 1024, 512, 512, 1024
+FLOPS = 2 * K * N * S
+
+F32 = mybir.dt.float32
+BF16 = mybir.dt.bfloat16
+I32 = mybir.dt.int32
+U32 = mybir.dt.uint32
+U16 = mybir.dt.uint16
+U8 = mybir.dt.uint8
+FP8X4 = mybir.dt.float8_e4m3fn_x4
+
+P = 128
+PACK = 4
+STRIPE = 16
+QUADS = 4
+ROW_ORDER = (2, 0, 1, 3)
+HALF = S // 2
+VECTOR_COLS = 512
+VECTOR_M = 44
+CHUNK = 256
+LEAD = 128
+
+
+def tile_picked_kvput_none_po_kernel(
+    tc, x_words, x_scales, mem, w1, offs, slot, out_0, out_1, out_2
+):
+    nc = tc.nc
+    first, last = ROW_ORDER[0], ROW_ORDER[-1]
+    mem_rows = mem.rearrange("(p t) c -> p t c", t=PACK)
+    out_rows = out_0.rearrange("(p t) c -> p t c", t=PACK)
+    w_rows = w1.rearrange("(p j) n -> p j n", j=PACK)
+    out_words = out_1[0].rearrange("p c r -> p (c r)").bitcast(I32)
+
+    with ExitStack() as ctx:
+        keep = ctx.enter_context(tc.tile_pool(name="keep", bufs=1))
+        psum = ctx.enter_context(tc.psum_pool(name="psum", bufs=1))
+
+        offs_sb = keep.tile([P, S // STRIPE], U16, name="offs_sb")
+        slot_sb = keep.tile([P, S // STRIPE], U16, name="slot_sb")
+        xs_all = keep.tile([P, T], U8, name="xs_all", align_bytes=64)
+        xw_all = keep.tile([P, T], U32, name="xw_all", align_bytes=64)
+        w_raw = [keep.tile([P, PACK, N // 2], F32, name=f"w_raw{h}", align_bytes=64) for h in range(2)]
+        store = [keep.tile([P, U], F32, name=f"store{t}", align_bytes=64) for t in range(PACK)]
+
+        nc.vector.memset(xs_all[:].bitcast(I32), 0)
+        nc.sync.dma_start(xw_all[:].bitcast(I32), x_words[0].rearrange("p c r -> p (c r)").bitcast(I32))
+        nc.sync.dma_start(offs_sb[:], offs)
+        nc.sync.dma_start(w_raw[0][:], w_rows[:, :, : N // 2])
+        for q in range(QUADS):
+            nc.sync.dma_start(
+                xs_all[32 * q : 32 * q + 4, :].bitcast(I32), x_scales[0][4 * q : 4 * q + 4, :].bitcast(I32)
+            )
+        nc.sync.dma_start(w_raw[1][:], w_rows[:, :, N // 2 :])
+        nc.sync.dma_start(store[first][:], mem_rows[:, first, :])
+        nc.sync.dma_start(slot_sb[:], slot)
+        for t in ROW_ORDER[1:]:
+            nc.sync.dma_start(store[t][:], mem_rows[:, t, :])
+
+        xs = keep.tile([P, S], U8, name="xs", align_bytes=64)
+        xw = keep.tile([P, S], U32, name="xw", align_bytes=64)
+        nc.vector.tensor_copy(xw[:], xw_all[:].indirect(offs_sb[:]))
+        nc.vector.tensor_copy(xs[:], xs_all[:].indirect(offs_sb[:]))
+
+        w_bf = keep.tile([P, PACK, P, PACK], BF16, name="w_bf", align_bytes=64)
+        w_dealt = w_bf[:].rearrange("p t m j -> p m j t")
+        half_m = P // 2
+        nc.scalar.copy(w_dealt[:, :half_m], w_raw[0][:].rearrange("p j (m t) -> p m j t", t=PACK))
+        w_late = w_raw[1][:].rearrange("p j (m t) -> p m j t", t=PACK)
+        nc.vector.tensor_copy(w_dealt[:, half_m : half_m + VECTOR_M], w_late[:, :VECTOR_M])
+        nc.scalar.copy(w_dealt[:, half_m + VECTOR_M :], w_late[:, VECTOR_M:])
+
+        ww = [keep.tile([P, P], U32, name=f"ww{t}", align_bytes=64) for t in range(PACK)]
+        ws = [keep.tile([P, P], U8, name=f"ws{t}", align_bytes=64) for t in range(PACK)]
+
+        def quantise_w(t):
+            nc.vector.quantize_mx(
+                out=ww[t][:].bitcast(FP8X4),
+                scales=ws[t][:],
+                in_=w_bf[:, t].rearrange("p m j -> p (m j)"),
+            )
+
+        y = [keep.tile([P, S], F32, name=f"y{t}", align_bytes=64) for t in range(PACK)]
+
+        def project(t, lo, hi):
+            acc = psum.tile([P, hi - lo], F32, name=f"acc{t}_{lo}")
+            nc.tensor.matmul_mx(
+                out=acc[:],
+                lhsT=ww[t][:].bitcast(FP8X4),
+                lhsT_scale=ws[t][:],
+                rhs=xw[:, lo:hi].bitcast(FP8X4),
+                rhs_scale=xs[:, lo:hi],
+                start=True,
+                stop=True,
+            )
+            nc.scalar.copy(y[t][:, lo:hi], acc[:])
+
+        def scatter(t, lo, hi):
+            nc.vector.tensor_copy(store[t][:].indirect(slot_sb[:, lo // STRIPE : hi // STRIPE]), y[t][:, lo:hi])
+
+        quantise_w(first)
+        for lo, hi in ((0, LEAD), (LEAD, HALF), (HALF, S)):
+            project(first, lo, hi)
+        for t in ROW_ORDER[1:]:
+            quantise_w(t)
+            project(t, 0, S)
+
+        out_bf = keep.tile([P, U, PACK], BF16, name="out_bf", align_bytes=64)
+        codes = keep.tile([P, U], U32, name="codes", align_bytes=64)
+        scales = keep.tile([P, U], U8, name="scales", align_bytes=64)
+
+        scatter(first, 0, LEAD)
+        scatter(first, LEAD, S)
+        nc.sync.dma_start(out_rows[:, first, :], store[first][:])
+        nc.scalar.copy(
+            out_bf[:, :VECTOR_COLS, first : first + 2],
+            store[first][:, :VECTOR_COLS].unsqueeze(2).to_broadcast([P, VECTOR_COLS, 2]),
+        )
+        nc.scalar.copy(out_bf[:, VECTOR_COLS:, first], store[first][:, VECTOR_COLS:])
+        for t in ROW_ORDER[1:-1]:
+            scatter(t, 0, S)
+            nc.sync.dma_start(out_rows[:, t, :], store[t][:])
+            for lo in range(0, U, 2 * CHUNK):
+                nc.scalar.copy(out_bf[:, lo : lo + 2 * CHUNK, t], store[t][:, lo : lo + 2 * CHUNK])
+        scatter(last, 0, S)
+        nc.sync.dma_start(out_rows[:, last, :], store[last][:])
+        for lo in range(0, U, CHUNK):
+            copy = nc.vector.tensor_copy if lo < VECTOR_COLS else nc.scalar.copy
+            copy(out_bf[:, lo : lo + CHUNK, last], store[last][:, lo : lo + CHUNK])
+
+        stored = 0
+        for lo in range(0, U, CHUNK):
+            hi = lo + CHUNK
+            nc.vector.quantize_mx(
+                out=codes[:, lo:hi].bitcast(FP8X4),
+                scales=scales[:, lo:hi],
+                in_=out_bf[:, lo:hi, :].rearrange("p c t -> p (c t)"),
+            )
+            if hi >= VECTOR_COLS:
+                nc.sync.dma_start(out_words[:, stored:hi], codes[:, stored:hi].bitcast(I32))
+                stored = hi
+        for q in range(QUADS):
+            queue = nc.scalar if q % 2 == 0 else nc.sync
+            queue.dma_start(
+                out_2[0][4 * q : 4 * q + 4, :].bitcast(I32), scales[32 * q : 32 * q + 4, :].bitcast(I32)
+            )

@@ -17,10 +17,10 @@ P = 128
 PACK = 4
 STRIPE = 16
 QUADS = 4
-ROW_ORDER = (2, 0, 1, 3)
+ROW_ORDER = (0, 2, 3, 1)
 HALF = S // 2
 VECTOR_COLS = 512
-VECTOR_M = 44
+VECTOR_M = 64
 CHUNK = 256
 LEAD = 128
 
@@ -43,18 +43,18 @@ def tile_picked_kvput_none_po_kernel(
         slot_sb = keep.tile([P, S // STRIPE], U16, name="slot_sb")
         xs_all = keep.tile([P, T], U8, name="xs_all", align_bytes=64)
         xw_all = keep.tile([P, T], U32, name="xw_all", align_bytes=64)
-        w_raw = [keep.tile([P, PACK, N // 2], F32, name=f"w_raw{h}", align_bytes=64) for h in range(2)]
+        w_raw = [keep.tile([P, 2, N], F32, name=f"w_raw{h}", align_bytes=64) for h in range(2)]
         store = [keep.tile([P, U], F32, name=f"store{t}", align_bytes=64) for t in range(PACK)]
 
         nc.vector.memset(xs_all[:].bitcast(I32), 0)
-        nc.sync.dma_start(xw_all[:].bitcast(I32), x_words[0].rearrange("p c r -> p (c r)").bitcast(I32))
+        nc.sync.dma_start(w_raw[0][:], w_rows[:, :2, :])
         nc.sync.dma_start(offs_sb[:], offs)
-        nc.sync.dma_start(w_raw[0][:], w_rows[:, :, : N // 2])
         for q in range(QUADS):
             nc.sync.dma_start(
                 xs_all[32 * q : 32 * q + 4, :].bitcast(I32), x_scales[0][4 * q : 4 * q + 4, :].bitcast(I32)
             )
-        nc.sync.dma_start(w_raw[1][:], w_rows[:, :, N // 2 :])
+        nc.sync.dma_start(xw_all[:].bitcast(I32), x_words[0].rearrange("p c r -> p (c r)").bitcast(I32))
+        nc.sync.dma_start(w_raw[1][:], w_rows[:, 2:, :])
         nc.sync.dma_start(store[first][:], mem_rows[:, first, :])
         nc.sync.dma_start(slot_sb[:], slot)
         for t in ROW_ORDER[1:]:
@@ -62,16 +62,17 @@ def tile_picked_kvput_none_po_kernel(
 
         xs = keep.tile([P, S], U8, name="xs", align_bytes=64)
         xw = keep.tile([P, S], U32, name="xw", align_bytes=64)
-        nc.vector.tensor_copy(xw[:], xw_all[:].indirect(offs_sb[:]))
         nc.vector.tensor_copy(xs[:], xs_all[:].indirect(offs_sb[:]))
+        nc.vector.tensor_copy(xw[:], xw_all[:].indirect(offs_sb[:]))
 
         w_bf = keep.tile([P, PACK, P, PACK], BF16, name="w_bf", align_bytes=64)
-        w_dealt = w_bf[:].rearrange("p t m j -> p m j t")
-        half_m = P // 2
-        nc.scalar.copy(w_dealt[:, :half_m], w_raw[0][:].rearrange("p j (m t) -> p m j t", t=PACK))
-        w_late = w_raw[1][:].rearrange("p j (m t) -> p m j t", t=PACK)
-        nc.vector.tensor_copy(w_dealt[:, half_m : half_m + VECTOR_M], w_late[:, :VECTOR_M])
-        nc.scalar.copy(w_dealt[:, half_m + VECTOR_M :], w_late[:, VECTOR_M:])
+        w_dealt = w_bf[:].rearrange("p t m j -> p m t j")
+        w_early, w_late = (w[:].rearrange("p j (m t) -> p m t j", t=PACK) for w in w_raw)
+        nc.scalar.copy(w_dealt[:, :, :, :2], w_early)
+        nc.vector.tensor_copy(w_dealt[:, :, first, 2:], w_late[:, :, first])
+        rest = slice(first + 1, PACK)
+        nc.vector.tensor_copy(w_dealt[:, :VECTOR_M, rest, 2:], w_late[:, :VECTOR_M, rest])
+        nc.scalar.copy(w_dealt[:, VECTOR_M:, rest, 2:], w_late[:, VECTOR_M:, rest])
 
         ww = [keep.tile([P, P], U32, name=f"ww{t}", align_bytes=64) for t in range(PACK)]
         ws = [keep.tile([P, P], U8, name=f"ws{t}", align_bytes=64) for t in range(PACK)]

@@ -116,11 +116,8 @@ def tile_picked_kvput_none_po_kernel(
         scatter(first, 0, LEAD)
         scatter(first, LEAD, S)
         nc.sync.dma_start(out_rows[:, first, :], store[first][:])
-        nc.scalar.copy(
-            out_bf[:, :VECTOR_COLS, first : first + 2],
-            store[first][:, :VECTOR_COLS].unsqueeze(2).to_broadcast([P, VECTOR_COLS, 2]),
-        )
-        nc.scalar.copy(out_bf[:, VECTOR_COLS:, first], store[first][:, VECTOR_COLS:])
+        nc.scalar.copy(out_bf[:, 2:, first], store[first][:, 2:])
+        nc.scalar.copy(out_bf[:, :2, first : first + 2], store[first][:, :2].unsqueeze(2).to_broadcast([P, 2, 2]))
         for t in ROW_ORDER[1:-1]:
             scatter(t, 0, S)
             nc.sync.dma_start(out_rows[:, t, :], store[t][:])

@@ -18,11 +18,10 @@ PACK = 4
 STRIPE = 16
 QUADS = 4
 ROW_ORDER = (0, 2, 3, 1)
-HALF = S // 2
 VECTOR_COLS = 512
-VECTOR_M = 64
 CHUNK = 256
 LEAD = 128
+QUANTISED = ((0, 256), (256, 512), (512, 768), (768, 896), (896, 1024))
 
 
 def tile_picked_kvput_none_po_kernel(
@@ -32,7 +31,7 @@ def tile_picked_kvput_none_po_kernel(
     first, last = ROW_ORDER[0], ROW_ORDER[-1]
     mem_rows = mem.rearrange("(p t) c -> p t c", t=PACK)
     out_rows = out_0.rearrange("(p t) c -> p t c", t=PACK)
-    w_rows = w1.rearrange("(p j) n -> p j n", j=PACK)
+    w_rows = w1.rearrange("(p j) n -> p (j n)", j=PACK)
     out_words = out_1[0].rearrange("p c r -> p (c r)").bitcast(I32)
 
     with ExitStack() as ctx:
@@ -43,46 +42,48 @@ def tile_picked_kvput_none_po_kernel(
         slot_sb = keep.tile([P, S // STRIPE], U16, name="slot_sb")
         xs_all = keep.tile([P, T], U8, name="xs_all", align_bytes=64)
         xw_all = keep.tile([P, T], U32, name="xw_all", align_bytes=64)
-        w_raw = [keep.tile([P, 2, N], F32, name=f"w_raw{h}", align_bytes=64) for h in range(2)]
+        w_raw = keep.tile([P, PACK * N], F32, name="w_raw", align_bytes=64)
         store = [keep.tile([P, U], F32, name=f"store{t}", align_bytes=64) for t in range(PACK)]
 
         nc.vector.memset(xs_all[:].bitcast(I32), 0)
-        nc.sync.dma_start(w_raw[0][:], w_rows[:, :2, :])
         nc.sync.dma_start(offs_sb[:], offs)
+        nc.sync.dma_start(w_raw[:, : 2 * N], w_rows[:, : 2 * N])
         for q in range(QUADS):
             nc.sync.dma_start(
                 xs_all[32 * q : 32 * q + 4, :].bitcast(I32), x_scales[0][4 * q : 4 * q + 4, :].bitcast(I32)
             )
+        nc.sync.dma_start(w_raw[:, 2 * N :], w_rows[:, 2 * N :])
         nc.sync.dma_start(xw_all[:].bitcast(I32), x_words[0].rearrange("p c r -> p (c r)").bitcast(I32))
-        nc.sync.dma_start(w_raw[1][:], w_rows[:, 2:, :])
         nc.sync.dma_start(store[first][:], mem_rows[:, first, :])
         nc.sync.dma_start(slot_sb[:], slot)
         for t in ROW_ORDER[1:]:
             nc.sync.dma_start(store[t][:], mem_rows[:, t, :])
 
         xs = keep.tile([P, S], U8, name="xs", align_bytes=64)
+        pieces = ((0, LEAD), (LEAD, S - LEAD), (S - LEAD, S))
         xw = keep.tile([P, S], U32, name="xw", align_bytes=64)
         nc.vector.tensor_copy(xs[:], xs_all[:].indirect(offs_sb[:]))
-        nc.vector.tensor_copy(xw[:], xw_all[:].indirect(offs_sb[:]))
 
-        w_bf = keep.tile([P, PACK, P, PACK], BF16, name="w_bf", align_bytes=64)
-        w_dealt = w_bf[:].rearrange("p t m j -> p m t j")
-        w_early, w_late = (w[:].rearrange("p j (m t) -> p m t j", t=PACK) for w in w_raw)
-        nc.scalar.copy(w_dealt[:, :, :, :2], w_early)
-        nc.vector.tensor_copy(w_dealt[:, :, first, 2:], w_late[:, :, first])
-        rest = slice(first + 1, PACK)
-        nc.vector.tensor_copy(w_dealt[:, :VECTOR_M, rest, 2:], w_late[:, :VECTOR_M, rest])
-        nc.scalar.copy(w_dealt[:, VECTOR_M:, rest, 2:], w_late[:, VECTOR_M:, rest])
+        w_bf = keep.tile([P, 2, 2, P, PACK], BF16, name="w_bf", align_bytes=64)
+        w_even, w_odd = (w_bf[:, b].rearrange("p a m j -> p m a j") for b in range(2))
+        w_all = w_raw[:].rearrange("p (j m t) -> p m t j", j=PACK, t=PACK)
+        w_early = w_raw[:, : 2 * N].rearrange("p (j m t) -> p m t j", j=2, t=PACK)
+        w_late = w_raw[:, 2 * N :].rearrange("p (j m t) -> p m t j", j=2, t=PACK)
+        nc.scalar.copy(w_even[:, :, 0, :2], w_early[:, :, 0])
+        nc.vector.tensor_copy(w_even[:, :, 1, :2], w_early[:, :, 2])
+        nc.scalar.copy(w_even[:, :, 0, 2:], w_late[:, :, 0])
+        nc.vector.tensor_copy(w_even[:, :, 1, 2:], w_late[:, :, 2])
+        nc.scalar.copy(w_odd, w_all[:, :, 1::2])
 
-        ww = [keep.tile([P, P], U32, name=f"ww{t}", align_bytes=64) for t in range(PACK)]
-        ws = [keep.tile([P, P], U8, name=f"ws{t}", align_bytes=64) for t in range(PACK)]
+        ww, ws = {}, {}
 
-        def quantise_w(t):
-            nc.vector.quantize_mx(
-                out=ww[t][:].bitcast(FP8X4),
-                scales=ws[t][:],
-                in_=w_bf[:, t].rearrange("p m j -> p (m j)"),
-            )
+        def quantise_w(planes, rounded, scale_tag):
+            width = len(planes) * P
+            words = keep.tile([P, width], U32, name=f"ww{planes[0]}", align_bytes=64)
+            scale = keep.tile([P, width], U8, name=f"ws{planes[0]}", tag=scale_tag, align_bytes=64)
+            nc.vector.quantize_mx(out=words[:].bitcast(FP8X4), scales=scale[:], in_=rounded)
+            for i, t in enumerate(planes):
+                ww[t], ws[t] = words[:, i * P : (i + 1) * P], scale[:, i * P : (i + 1) * P]
 
         y = [keep.tile([P, S], F32, name=f"y{t}", align_bytes=64) for t in range(PACK)]
 
@@ -90,8 +91,8 @@ def tile_picked_kvput_none_po_kernel(
             acc = psum.tile([P, hi - lo], F32, name=f"acc{t}_{lo}")
             nc.tensor.matmul_mx(
                 out=acc[:],
-                lhsT=ww[t][:].bitcast(FP8X4),
-                lhsT_scale=ws[t][:],
+                lhsT=ww[t].bitcast(FP8X4),
+                lhsT_scale=ws[t],
                 rhs=xw[:, lo:hi].bitcast(FP8X4),
                 rhs_scale=xs[:, lo:hi],
                 start=True,
@@ -102,18 +103,21 @@ def tile_picked_kvput_none_po_kernel(
         def scatter(t, lo, hi):
             nc.vector.tensor_copy(store[t][:].indirect(slot_sb[:, lo // STRIPE : hi // STRIPE]), y[t][:, lo:hi])
 
-        quantise_w(first)
-        for lo, hi in ((0, LEAD), (LEAD, HALF), (HALF, S)):
+        quantise_w((0,), w_bf[:, 0, 0].rearrange("p m j -> p (m j)"), "ws_first")
+        quantise_w((2,), w_bf[:, 0, 1].rearrange("p m j -> p (m j)"), "ws_second")
+        for lo, hi in pieces:
+            nc.vector.tensor_copy(xw[:, lo:hi], xw_all[:].indirect(offs_sb[:, lo // STRIPE : hi // STRIPE]))
             project(first, lo, hi)
-        for t in ROW_ORDER[1:]:
-            quantise_w(t)
-            project(t, 0, S)
+        project(ROW_ORDER[1], 0, S)
 
         out_bf = keep.tile([P, U, PACK], BF16, name="out_bf", align_bytes=64)
         codes = keep.tile([P, U], U32, name="codes", align_bytes=64)
         scales = keep.tile([P, U], U8, name="scales", align_bytes=64)
 
         scatter(first, 0, LEAD)
+        quantise_w((1, 3), w_bf[:, 1].rearrange("p a m j -> p (a m j)"), "ws_third")
+        for t in ROW_ORDER[2:]:
+            project(t, 0, S)
         scatter(first, LEAD, S)
         nc.sync.dma_start(out_rows[:, first, :], store[first][:])
         nc.scalar.copy(out_bf[:, 2:, first], store[first][:, 2:])
@@ -125,19 +129,18 @@ def tile_picked_kvput_none_po_kernel(
                 nc.scalar.copy(out_bf[:, lo : lo + 2 * CHUNK, t], store[t][:, lo : lo + 2 * CHUNK])
         scatter(last, 0, S)
         nc.sync.dma_start(out_rows[:, last, :], store[last][:])
-        for lo in range(0, U, CHUNK):
+        for lo, hi in QUANTISED:
             copy = nc.vector.tensor_copy if lo < VECTOR_COLS else nc.scalar.copy
-            copy(out_bf[:, lo : lo + CHUNK, last], store[last][:, lo : lo + CHUNK])
+            copy(out_bf[:, lo:hi, last], store[last][:, lo:hi])
 
         stored = 0
-        for lo in range(0, U, CHUNK):
-            hi = lo + CHUNK
+        for lo, hi in QUANTISED:
             nc.vector.quantize_mx(
                 out=codes[:, lo:hi].bitcast(FP8X4),
                 scales=scales[:, lo:hi],
                 in_=out_bf[:, lo:hi, :].rearrange("p c t -> p (c t)"),
             )
-            if hi >= VECTOR_COLS:
+            if hi in (VECTOR_COLS, 768, U):
                 nc.sync.dma_start(out_words[:, stored:hi], codes[:, stored:hi].bitcast(I32))
                 stored = hi
         for q in range(QUADS):

@@ -46,11 +46,11 @@ def tile_picked_kvput_none_po_kernel(
         store = [keep.tile([P, U], F32, name=f"store{t}", align_bytes=64) for t in range(PACK)]
 
         nc.vector.memset(xs_all[:].bitcast(I32), 0)
-        nc.sync.dma_start(offs_sb[:], offs)
         nc.sync.dma_start(w_raw[:, : 2 * N], w_rows[:, : 2 * N])
+        nc.sync.dma_start(offs_sb[:], offs)
         for q in range(QUADS):
             nc.sync.dma_start(
-                xs_all[32 * q : 32 * q + 4, :].bitcast(I32), x_scales[0][4 * q : 4 * q + 4, :].bitcast(I32)
+                xs_all[q:P:32, :].bitcast(I32), x_scales[0][q:16:4, :].bitcast(I32)
             )
         nc.sync.dma_start(w_raw[:, 2 * N :], w_rows[:, 2 * N :])
         nc.sync.dma_start(xw_all[:].bitcast(I32), x_words[0].rearrange("p c r -> p (c r)").bitcast(I32))
@@ -140,11 +140,11 @@ def tile_picked_kvput_none_po_kernel(
                 scales=scales[:, lo:hi],
                 in_=out_bf[:, lo:hi, :].rearrange("p c t -> p (c t)"),
             )
-            if hi in (VECTOR_COLS, 768, U):
+            if hi in (VECTOR_COLS, 896, U):
                 nc.sync.dma_start(out_words[:, stored:hi], codes[:, stored:hi].bitcast(I32))
                 stored = hi
         for q in range(QUADS):
             queue = nc.scalar if q % 2 == 0 else nc.sync
             queue.dma_start(
-                out_2[0][4 * q : 4 * q + 4, :].bitcast(I32), scales[32 * q : 32 * q + 4, :].bitcast(I32)
+                out_2[0][q:16:4, :].bitcast(I32), scales[q:P:32, :].bitcast(I32)
             )

@@ -70,9 +70,9 @@ def tile_picked_kvput_none_po_kernel(
         w_early = w_raw[:, : 2 * N].rearrange("p (j m t) -> p m t j", j=2, t=PACK)
         w_late = w_raw[:, 2 * N :].rearrange("p (j m t) -> p m t j", j=2, t=PACK)
         nc.scalar.copy(w_even[:, :, 0, :2], w_early[:, :, 0])
-        nc.vector.tensor_copy(w_even[:, :, 1, :2], w_early[:, :, 2])
+        nc.gpsimd.tensor_copy(w_even[:, :, 1, :2], w_early[:, :, 2])
         nc.scalar.copy(w_even[:, :, 0, 2:], w_late[:, :, 0])
-        nc.vector.tensor_copy(w_even[:, :, 1, 2:], w_late[:, :, 2])
+        nc.gpsimd.tensor_copy(w_even[:, :, 1, 2:], w_late[:, :, 2])
         nc.scalar.copy(w_odd, w_all[:, :, 1::2])
 
         ww, ws = {}, {}

@@ -16,19 +16,23 @@ FP8X4 = mybir.dt.float8_e4m3fn_x4
 P = 128
 PACK = 4
 STRIPE = 16
-QUADS = 4
-ROW_ORDER = (0, 2, 3, 1)
-VECTOR_COLS = 512
-CHUNK = 256
+QUADRANT = 32
+SCALE_ROWS = 16
+
+PLANE_ORDER = (0, 2, 3, 1)
 LEAD = 128
+PIECES = ((0, LEAD), (LEAD, S - LEAD), (S - LEAD, S))
+SCALAR_COLS = 768
+VECTOR_COLS = 512
 QUANTISED = ((0, 256), (256, 512), (512, 768), (768, 896), (896, 1024))
+STORE_ENDS = (512, 896, 1024)
 
 
 def tile_picked_kvput_none_po_kernel(
     tc, x_words, x_scales, mem, w1, offs, slot, out_0, out_1, out_2
 ):
     nc = tc.nc
-    first, last = ROW_ORDER[0], ROW_ORDER[-1]
+    first, second, third, last = PLANE_ORDER
     mem_rows = mem.rearrange("(p t) c -> p t c", t=PACK)
     out_rows = out_0.rearrange("(p t) c -> p t c", t=PACK)
     w_rows = w1.rearrange("(p j) n -> p (j n)", j=PACK)
@@ -43,24 +47,22 @@ def tile_picked_kvput_none_po_kernel(
         xs_all = keep.tile([P, T], U8, name="xs_all", align_bytes=64)
         xw_all = keep.tile([P, T], U32, name="xw_all", align_bytes=64)
         w_raw = keep.tile([P, PACK * N], F32, name="w_raw", align_bytes=64)
-        store = [keep.tile([P, U], F32, name=f"store{t}", align_bytes=64) for t in range(PACK)]
+        plane = [keep.tile([P, U], F32, name=f"plane{t}", align_bytes=64) for t in range(PACK)]
 
         nc.vector.memset(xs_all[:].bitcast(I32), 0)
+
         nc.sync.dma_start(w_raw[:, : 2 * N], w_rows[:, : 2 * N])
         nc.sync.dma_start(offs_sb[:], offs)
-        for q in range(QUADS):
-            nc.sync.dma_start(
-                xs_all[q:P:32, :].bitcast(I32), x_scales[0][q:16:4, :].bitcast(I32)
-            )
+        for r in range(PACK):
+            nc.sync.dma_start(xs_all[r:P:QUADRANT, :].bitcast(I32), x_scales[0][r:SCALE_ROWS:PACK, :].bitcast(I32))
         nc.sync.dma_start(w_raw[:, 2 * N :], w_rows[:, 2 * N :])
         nc.sync.dma_start(xw_all[:].bitcast(I32), x_words[0].rearrange("p c r -> p (c r)").bitcast(I32))
-        nc.sync.dma_start(store[first][:], mem_rows[:, first, :])
+        nc.sync.dma_start(plane[first][:], mem_rows[:, first, :])
         nc.sync.dma_start(slot_sb[:], slot)
-        for t in ROW_ORDER[1:]:
-            nc.sync.dma_start(store[t][:], mem_rows[:, t, :])
+        for t in PLANE_ORDER[1:]:
+            nc.sync.dma_start(plane[t][:], mem_rows[:, t, :])
 
         xs = keep.tile([P, S], U8, name="xs", align_bytes=64)
-        pieces = ((0, LEAD), (LEAD, S - LEAD), (S - LEAD, S))
         xw = keep.tile([P, S], U32, name="xw", align_bytes=64)
         nc.vector.tensor_copy(xs[:], xs_all[:].indirect(offs_sb[:]))
 
@@ -75,24 +77,22 @@ def tile_picked_kvput_none_po_kernel(
         nc.gpsimd.tensor_copy(w_even[:, :, 1, 2:], w_late[:, :, 2])
         nc.scalar.copy(w_odd, w_all[:, :, 1::2])
 
-        ww, ws = {}, {}
+        w_words, w_scales, y = {}, {}, {}
 
-        def quantise_w(planes, rounded, scale_tag):
+        def quantise_w(planes, rounded):
             width = len(planes) * P
-            words = keep.tile([P, width], U32, name=f"ww{planes[0]}", align_bytes=64)
-            scale = keep.tile([P, width], U8, name=f"ws{planes[0]}", tag=scale_tag, align_bytes=64)
+            words = keep.tile([P, width], U32, name=f"w_words{planes[0]}", align_bytes=64)
+            scale = keep.tile([P, width], U8, name=f"w_scales{planes[0]}", align_bytes=64)
             nc.vector.quantize_mx(out=words[:].bitcast(FP8X4), scales=scale[:], in_=rounded)
             for i, t in enumerate(planes):
-                ww[t], ws[t] = words[:, i * P : (i + 1) * P], scale[:, i * P : (i + 1) * P]
-
-        y = [keep.tile([P, S], F32, name=f"y{t}", align_bytes=64) for t in range(PACK)]
+                w_words[t], w_scales[t] = words[:, i * P : (i + 1) * P], scale[:, i * P : (i + 1) * P]
 
         def project(t, lo, hi):
             acc = psum.tile([P, hi - lo], F32, name=f"acc{t}_{lo}")
             nc.tensor.matmul_mx(
                 out=acc[:],
-                lhsT=ww[t].bitcast(FP8X4),
-                lhsT_scale=ws[t],
+                lhsT=w_words[t].bitcast(FP8X4),
+                lhsT_scale=w_scales[t],
                 rhs=xw[:, lo:hi].bitcast(FP8X4),
                 rhs_scale=xs[:, lo:hi],
                 start=True,
@@ -101,37 +101,42 @@ def tile_picked_kvput_none_po_kernel(
             nc.scalar.copy(y[t][:, lo:hi], acc[:])
 
         def scatter(t, lo, hi):
-            nc.vector.tensor_copy(store[t][:].indirect(slot_sb[:, lo // STRIPE : hi // STRIPE]), y[t][:, lo:hi])
+            nc.vector.tensor_copy(plane[t][:].indirect(slot_sb[:, lo // STRIPE : hi // STRIPE]), y[t][:, lo:hi])
 
-        quantise_w((0,), w_bf[:, 0, 0].rearrange("p m j -> p (m j)"), "ws_first")
-        quantise_w((2,), w_bf[:, 0, 1].rearrange("p m j -> p (m j)"), "ws_second")
-        for lo, hi in pieces:
+        for t in (first, second, third):
+            y[t] = keep.tile([P, S], F32, name=f"y{t}", tag=f"y{t}", align_bytes=64)
+        quantise_w((0,), w_bf[:, 0, 0].rearrange("p m j -> p (m j)"))
+        quantise_w((2,), w_bf[:, 0, 1].rearrange("p m j -> p (m j)"))
+        for lo, hi in PIECES:
             nc.vector.tensor_copy(xw[:, lo:hi], xw_all[:].indirect(offs_sb[:, lo // STRIPE : hi // STRIPE]))
             project(first, lo, hi)
-        project(ROW_ORDER[1], 0, S)
+        project(second, 0, S)
 
         out_bf = keep.tile([P, U, PACK], BF16, name="out_bf", align_bytes=64)
         codes = keep.tile([P, U], U32, name="codes", align_bytes=64)
         scales = keep.tile([P, U], U8, name="scales", align_bytes=64)
 
         scatter(first, 0, LEAD)
-        quantise_w((1, 3), w_bf[:, 1].rearrange("p a m j -> p (a m j)"), "ws_third")
-        for t in ROW_ORDER[2:]:
-            project(t, 0, S)
+        quantise_w((1, 3), w_bf[:, 1].rearrange("p a m j -> p (a m j)"))
+        project(third, 0, S)
         scatter(first, LEAD, S)
-        nc.sync.dma_start(out_rows[:, first, :], store[first][:])
-        nc.scalar.copy(out_bf[:, 2:, first], store[first][:, 2:])
-        nc.scalar.copy(out_bf[:, :2, first : first + 2], store[first][:, :2].unsqueeze(2).to_broadcast([P, 2, 2]))
-        for t in ROW_ORDER[1:-1]:
+        nc.sync.dma_start(out_rows[:, first, :], plane[first][:])
+        nc.scalar.copy(out_bf[:, :, first], plane[first][:])
+
+        y[last] = keep.tile([P, S], F32, name=f"y{last}", tag=f"y{first}", align_bytes=64)
+        project(last, 0, S)
+
+        for t in (second, third):
             scatter(t, 0, S)
-            nc.sync.dma_start(out_rows[:, t, :], store[t][:])
-            for lo in range(0, U, 2 * CHUNK):
-                nc.scalar.copy(out_bf[:, lo : lo + 2 * CHUNK, t], store[t][:, lo : lo + 2 * CHUNK])
+            nc.sync.dma_start(out_rows[:, t, :], plane[t][:])
+            nc.scalar.copy(out_bf[:, :SCALAR_COLS, t], plane[t][:, :SCALAR_COLS])
+            nc.gpsimd.tensor_copy(out_bf[:, SCALAR_COLS:, t], plane[t][:, SCALAR_COLS:])
+
         scatter(last, 0, S)
-        nc.sync.dma_start(out_rows[:, last, :], store[last][:])
+        nc.sync.dma_start(out_rows[:, last, :], plane[last][:])
         for lo, hi in QUANTISED:
             copy = nc.vector.tensor_copy if lo < VECTOR_COLS else nc.scalar.copy
-            copy(out_bf[:, lo:hi, last], store[last][:, lo:hi])
+            copy(out_bf[:, lo:hi, last], plane[last][:, lo:hi])
 
         stored = 0
         for lo, hi in QUANTISED:
@@ -140,11 +145,9 @@ def tile_picked_kvput_none_po_kernel(
                 scales=scales[:, lo:hi],
                 in_=out_bf[:, lo:hi, :].rearrange("p c t -> p (c t)"),
             )
-            if hi in (VECTOR_COLS, 896, U):
+            if hi in STORE_ENDS:
                 nc.sync.dma_start(out_words[:, stored:hi], codes[:, stored:hi].bitcast(I32))
                 stored = hi
-        for q in range(QUADS):
-            queue = nc.scalar if q % 2 == 0 else nc.sync
-            queue.dma_start(
-                out_2[0][q:16:4, :].bitcast(I32), scales[q:P:32, :].bitcast(I32)
-            )
+        for r in range(PACK):
+            queue = nc.scalar if r % 2 == 0 else nc.sync
+            queue.dma_start(out_2[0][r:SCALE_ROWS:PACK, :].bitcast(I32), scales[r:P:QUADRANT, :].bitcast(I32))

@@ -19,10 +19,10 @@ STRIPE = 16
 QUADRANT = 32
 SCALE_ROWS = 16
 
-PLANE_ORDER = (0, 2, 3, 1)
+PLANE_ORDER = (2, 0, 3, 1)
 LEAD = 128
 PIECES = ((0, LEAD), (LEAD, S - LEAD), (S - LEAD, S))
-SCALAR_COLS = 768
+SCALAR_COLS = 640
 VECTOR_COLS = 512
 QUANTISED = ((0, 256), (256, 512), (512, 768), (768, 896), (896, 1024))
 STORE_ENDS = (512, 896, 1024)
@@ -71,10 +71,10 @@ def tile_picked_kvput_none_po_kernel(
         w_all = w_raw[:].rearrange("p (j m t) -> p m t j", j=PACK, t=PACK)
         w_early = w_raw[:, : 2 * N].rearrange("p (j m t) -> p m t j", j=2, t=PACK)
         w_late = w_raw[:, 2 * N :].rearrange("p (j m t) -> p m t j", j=2, t=PACK)
-        nc.scalar.copy(w_even[:, :, 0, :2], w_early[:, :, 0])
-        nc.gpsimd.tensor_copy(w_even[:, :, 1, :2], w_early[:, :, 2])
-        nc.scalar.copy(w_even[:, :, 0, 2:], w_late[:, :, 0])
-        nc.gpsimd.tensor_copy(w_even[:, :, 1, 2:], w_late[:, :, 2])
+        nc.scalar.copy(w_even[:, :, 1, :2], w_early[:, :, 2])
+        nc.gpsimd.tensor_copy(w_even[:, :, 0, :2], w_early[:, :, 0])
+        nc.scalar.copy(w_even[:, :, 1, 2:], w_late[:, :, 2])
+        nc.gpsimd.tensor_copy(w_even[:, :, 0, 2:], w_late[:, :, 0])
         nc.scalar.copy(w_odd, w_all[:, :, 1::2])
 
         w_words, w_scales, y = {}, {}, {}
@@ -87,47 +87,52 @@ def tile_picked_kvput_none_po_kernel(
             for i, t in enumerate(planes):
                 w_words[t], w_scales[t] = words[:, i * P : (i + 1) * P], scale[:, i * P : (i + 1) * P]
 
-        def project(t, lo, hi):
-            acc = psum.tile([P, hi - lo], F32, name=f"acc{t}_{lo}")
-            nc.tensor.matmul_mx(
-                out=acc[:],
-                lhsT=w_words[t].bitcast(FP8X4),
-                lhsT_scale=w_scales[t],
-                rhs=xw[:, lo:hi].bitcast(FP8X4),
-                rhs_scale=xs[:, lo:hi],
-                start=True,
-                stop=True,
-            )
-            nc.scalar.copy(y[t][:, lo:hi], acc[:])
+        def project(t, *pieces, bank=None):
+            start, end = pieces[0][0], pieces[-1][1]
+            acc = psum.tile([P, end - start], F32, name=f"acc{t}_{start}", tag=bank or f"acc{t}_{start}")
+            for lo, hi in pieces:
+                nc.tensor.matmul_mx(
+                    out=acc[:, lo - start : hi - start],
+                    lhsT=w_words[t].bitcast(FP8X4),
+                    lhsT_scale=w_scales[t],
+                    rhs=xw[:, lo:hi].bitcast(FP8X4),
+                    rhs_scale=xs[:, lo:hi],
+                    start=True,
+                    stop=True,
+                )
+            nc.scalar.copy(y[t][:, start:end], acc[:])
 
         def scatter(t, lo, hi):
             nc.vector.tensor_copy(plane[t][:].indirect(slot_sb[:, lo // STRIPE : hi // STRIPE]), y[t][:, lo:hi])
 
         for t in (first, second, third):
             y[t] = keep.tile([P, S], F32, name=f"y{t}", tag=f"y{t}", align_bytes=64)
-        quantise_w((0,), w_bf[:, 0, 0].rearrange("p m j -> p (m j)"))
         quantise_w((2,), w_bf[:, 0, 1].rearrange("p m j -> p (m j)"))
+        quantise_w((0,), w_bf[:, 0, 0].rearrange("p m j -> p (m j)"))
         for lo, hi in PIECES:
             nc.vector.tensor_copy(xw[:, lo:hi], xw_all[:].indirect(offs_sb[:, lo // STRIPE : hi // STRIPE]))
-            project(first, lo, hi)
-        project(second, 0, S)
+            if lo == 0:
+                project(first, (lo, hi))
+            project(second, (lo, hi))
 
         out_bf = keep.tile([P, U, PACK], BF16, name="out_bf", align_bytes=64)
         codes = keep.tile([P, U], U32, name="codes", align_bytes=64)
         scales = keep.tile([P, U], U8, name="scales", align_bytes=64)
 
         scatter(first, 0, LEAD)
+        scatter(second, 0, S)
         quantise_w((1, 3), w_bf[:, 1].rearrange("p a m j -> p (a m j)"))
-        project(third, 0, S)
-        scatter(first, LEAD, S)
-        nc.sync.dma_start(out_rows[:, first, :], plane[first][:])
-        nc.scalar.copy(out_bf[:, :, first], plane[first][:])
+        project(third, (0, S), bank="late")
+        for piece in PIECES[1:]:
+            project(first, piece, bank="late")
+        nc.sync.dma_start(out_rows[:, second, :], plane[second][:])
+        nc.scalar.copy(out_bf[:, :, second], plane[second][:])
 
-        y[last] = keep.tile([P, S], F32, name=f"y{last}", tag=f"y{first}", align_bytes=64)
-        project(last, 0, S)
+        y[last] = keep.tile([P, S], F32, name=f"y{last}", tag=f"y{second}", align_bytes=64)
+        project(last, (0, S))
 
-        for t in (second, third):
-            scatter(t, 0, S)
+        for t, lo in ((first, LEAD), (third, 0)):
+            scatter(t, lo, S)
             nc.sync.dma_start(out_rows[:, t, :], plane[t][:])
             nc.scalar.copy(out_bf[:, :SCALAR_COLS, t], plane[t][:, :SCALAR_COLS])
             nc.gpsimd.tensor_copy(out_bf[:, SCALAR_COLS:, t], plane[t][:, SCALAR_COLS:])

@@ -24,8 +24,9 @@ LEAD = 128
 PIECES = ((0, LEAD), (LEAD, S - LEAD), (S - LEAD, S))
 SCALAR_COLS = 640
 VECTOR_COLS = 512
-QUANTISED = ((0, 256), (256, 512), (512, 768), (768, 896), (896, 1024))
-STORE_ENDS = (512, 896, 1024)
+ROUNDED = ((0, 256), (256, 512), (512, 768), (768, 896), (896, 1024))
+QUANTISED = ((0, 256), (256, 384), (384, 512), (512, 768), (768, 896), (896, 1024))
+STORE_ENDS = (384, 768, 1024)
 
 
 def tile_picked_kvput_none_po_kernel(
@@ -87,20 +88,18 @@ def tile_picked_kvput_none_po_kernel(
             for i, t in enumerate(planes):
                 w_words[t], w_scales[t] = words[:, i * P : (i + 1) * P], scale[:, i * P : (i + 1) * P]
 
-        def project(t, *pieces, bank=None):
-            start, end = pieces[0][0], pieces[-1][1]
-            acc = psum.tile([P, end - start], F32, name=f"acc{t}_{start}", tag=bank or f"acc{t}_{start}")
-            for lo, hi in pieces:
-                nc.tensor.matmul_mx(
-                    out=acc[:, lo - start : hi - start],
-                    lhsT=w_words[t].bitcast(FP8X4),
-                    lhsT_scale=w_scales[t],
-                    rhs=xw[:, lo:hi].bitcast(FP8X4),
-                    rhs_scale=xs[:, lo:hi],
-                    start=True,
-                    stop=True,
-                )
-            nc.scalar.copy(y[t][:, start:end], acc[:])
+        def project(t, lo, hi, bank):
+            acc = psum.tile([P, hi - lo], F32, name=f"acc{t}_{lo}", tag=bank)
+            nc.tensor.matmul_mx(
+                out=acc[:],
+                lhsT=w_words[t].bitcast(FP8X4),
+                lhsT_scale=w_scales[t],
+                rhs=xw[:, lo:hi].bitcast(FP8X4),
+                rhs_scale=xs[:, lo:hi],
+                start=True,
+                stop=True,
+            )
+            nc.scalar.copy(y[t][:, lo:hi], acc[:])
 
         def scatter(t, lo, hi):
             nc.vector.tensor_copy(plane[t][:].indirect(slot_sb[:, lo // STRIPE : hi // STRIPE]), y[t][:, lo:hi])
@@ -111,9 +110,9 @@ def tile_picked_kvput_none_po_kernel(
         quantise_w((0,), w_bf[:, 0, 0].rearrange("p m j -> p (m j)"))
         for lo, hi in PIECES:
             nc.vector.tensor_copy(xw[:, lo:hi], xw_all[:].indirect(offs_sb[:, lo // STRIPE : hi // STRIPE]))
-            if lo == 0:
-                project(first, (lo, hi))
-            project(second, (lo, hi))
+            if hi == LEAD:
+                project(first, lo, hi, bank="lead")
+            project(second, lo, hi, bank=f"second{lo}")
 
         out_bf = keep.tile([P, U, PACK], BF16, name="out_bf", align_bytes=64)
         codes = keep.tile([P, U], U32, name="codes", align_bytes=64)
@@ -122,14 +121,14 @@ def tile_picked_kvput_none_po_kernel(
         scatter(first, 0, LEAD)
         scatter(second, 0, S)
         quantise_w((1, 3), w_bf[:, 1].rearrange("p a m j -> p (a m j)"))
-        project(third, (0, S), bank="late")
-        for piece in PIECES[1:]:
-            project(first, piece, bank="late")
+        project(third, 0, S, bank="shared")
+        for lo, hi in PIECES[1:]:
+            project(first, lo, hi, bank="shared")
         nc.sync.dma_start(out_rows[:, second, :], plane[second][:])
         nc.scalar.copy(out_bf[:, :, second], plane[second][:])
 
         y[last] = keep.tile([P, S], F32, name=f"y{last}", tag=f"y{second}", align_bytes=64)
-        project(last, (0, S))
+        project(last, 0, S, bank="last")
 
         for t, lo in ((first, LEAD), (third, 0)):
             scatter(t, lo, S)
@@ -139,7 +138,7 @@ def tile_picked_kvput_none_po_kernel(
 
         scatter(last, 0, S)
         nc.sync.dma_start(out_rows[:, last, :], plane[last][:])
-        for lo, hi in QUANTISED:
+        for lo, hi in ROUNDED:
             copy = nc.vector.tensor_copy if lo < VECTOR_COLS else nc.scalar.copy
             copy(out_bf[:, lo:hi, last], plane[last][:, lo:hi])
 

@@ -12,18 +12,23 @@ U32 = mybir.dt.uint32
 U16 = mybir.dt.uint16
 U8 = mybir.dt.uint8
 FP8X4 = mybir.dt.float8_e4m3fn_x4
+MULT = mybir.AluOpType.mult
+ADD = mybir.AluOpType.add
 
 P = 128
+HALF = 64
 PACK = 4
 STRIPE = 16
 QUADRANT = 32
 SCALE_ROWS = 16
 
-PLANE_ORDER = (2, 0, 3, 1)
-LEAD = 128
-PIECES = ((0, LEAD), (LEAD, S - LEAD), (S - LEAD, S))
-SCALAR_COLS = 640
+LEAD = 256
+PIECES = ((0, 128), (128, 256), (256, 512))
+EARLY_J = 3
 VECTOR_COLS = 512
+PARK = 4
+GROUP = 128
+GP_COLS = 88
 ROUNDED = ((0, 256), (256, 512), (512, 768), (768, 896), (896, 1024))
 QUANTISED = ((0, 256), (256, 384), (384, 512), (512, 768), (768, 896), (896, 1024))
 STORE_ENDS = (384, 768, 1024)
@@ -33,11 +38,17 @@ def tile_picked_kvput_none_po_kernel(
     tc, x_words, x_scales, mem, w1, offs, slot, out_0, out_1, out_2
 ):
     nc = tc.nc
-    first, second, third, last = PLANE_ORDER
     mem_rows = mem.rearrange("(p t) c -> p t c", t=PACK)
     out_rows = out_0.rearrange("(p t) c -> p t c", t=PACK)
-    w_rows = w1.rearrange("(p j) n -> p (j n)", j=PACK)
+    w_rows = w1.rearrange("(p j) n -> p j n", j=PACK)
     out_words = out_1[0].rearrange("p c r -> p (c r)").bitcast(I32)
+    HN = N // 2
+    REST = S - LEAD
+    J = ((0, EARLY_J), (EARLY_J, PACK))
+    JH = ((0, 2), (2, PACK))
+
+    def rows_of(ap, i):
+        return ap[i * HALF : (i + 1) * HALF, 0:2, :] if i < 2 else ap[:, i, :]
 
     with ExitStack() as ctx:
         keep = ctx.enter_context(tc.tile_pool(name="keep", bufs=1))
@@ -46,112 +57,156 @@ def tile_picked_kvput_none_po_kernel(
         offs_sb = keep.tile([P, S // STRIPE], U16, name="offs_sb")
         slot_sb = keep.tile([P, S // STRIPE], U16, name="slot_sb")
         xs_all = keep.tile([P, T], U8, name="xs_all", align_bytes=64)
-        xw_all = keep.tile([P, T], U32, name="xw_all", align_bytes=64)
-        w_raw = keep.tile([P, PACK * N], F32, name="w_raw", align_bytes=64)
-        plane = [keep.tile([P, U], F32, name=f"plane{t}", align_bytes=64) for t in range(PACK)]
+        xw_all = keep.tile([P, T], U32, name="xw_all", tag="xw_all", align_bytes=64)
+        w_lo = [keep.tile([P, (b - a) * HN], F32, name=f"w_lo{a}", align_bytes=64)[:] for a, b in J]
+        w_hi_early = keep.tile([P, 2 * HN], F32, name="w_hi_early", align_bytes=64)
+        w_hi_late = keep.tile([P, 2 * HN], F32, name="w_hi_late", tag="late", align_bytes=64)
+        w_hi = [w_hi_early[:], w_hi_late[:]]
+        win = [keep.tile([P, U], F32, name=f"win{i}", align_bytes=64) for i in range(PACK)]
 
         nc.vector.memset(xs_all[:].bitcast(I32), 0)
 
-        nc.sync.dma_start(w_raw[:, : 2 * N], w_rows[:, : 2 * N])
+        def load_w(dst, h, cols, cut):
+            a, b = cut[h]
+            nc.sync.dma_start(dst[h].rearrange("p (j n) -> p j n", j=b - a), w_rows[:, a:b, cols])
+
+        load_w(w_lo, 0, slice(0, HN), J)
         nc.sync.dma_start(offs_sb[:], offs)
         for r in range(PACK):
             nc.sync.dma_start(xs_all[r:P:QUADRANT, :].bitcast(I32), x_scales[0][r:SCALE_ROWS:PACK, :].bitcast(I32))
-        nc.sync.dma_start(w_raw[:, 2 * N :], w_rows[:, 2 * N :])
+        load_w(w_lo, 1, slice(0, HN), J)
         nc.sync.dma_start(xw_all[:].bitcast(I32), x_words[0].rearrange("p c r -> p (c r)").bitcast(I32))
-        nc.sync.dma_start(plane[first][:], mem_rows[:, first, :])
+        nc.sync.dma_start(win[0][:], rows_of(mem_rows, 0))
         nc.sync.dma_start(slot_sb[:], slot)
-        for t in PLANE_ORDER[1:]:
-            nc.sync.dma_start(plane[t][:], mem_rows[:, t, :])
+        load_w(w_hi, 0, slice(HN, N), JH)
+        load_w(w_hi, 1, slice(HN, N), JH)
+        for i in range(1, PACK):
+            nc.sync.dma_start(win[i][:], rows_of(mem_rows, i))
 
         xs = keep.tile([P, S], U8, name="xs", align_bytes=64)
         xw = keep.tile([P, S], U32, name="xw", align_bytes=64)
         nc.vector.tensor_copy(xs[:], xs_all[:].indirect(offs_sb[:]))
 
-        w_bf = keep.tile([P, 2, 2, P, PACK], BF16, name="w_bf", align_bytes=64)
-        w_even, w_odd = (w_bf[:, b].rearrange("p a m j -> p m a j") for b in range(2))
-        w_all = w_raw[:].rearrange("p (j m t) -> p m t j", j=PACK, t=PACK)
-        w_early = w_raw[:, : 2 * N].rearrange("p (j m t) -> p m t j", j=2, t=PACK)
-        w_late = w_raw[:, 2 * N :].rearrange("p (j m t) -> p m t j", j=2, t=PACK)
-        nc.scalar.copy(w_even[:, :, 1, :2], w_early[:, :, 2])
-        nc.gpsimd.tensor_copy(w_even[:, :, 0, :2], w_early[:, :, 0])
-        nc.scalar.copy(w_even[:, :, 1, 2:], w_late[:, :, 2])
-        nc.gpsimd.tensor_copy(w_even[:, :, 0, 2:], w_late[:, :, 0])
-        nc.scalar.copy(w_odd, w_all[:, :, 1::2])
+        w_bf01 = [keep.tile([P, HALF, 2, PACK], BF16, name=f"w_bf{i}", align_bytes=64) for i in range(2)]
+        w_bf23 = [keep.tile([P, 2, HALF, PACK], BF16, name=f"w_bf23_{g}", align_bytes=64) for g in range(2)]
 
-        w_words, w_scales, y = {}, {}, {}
+        def round_w(raw, g, h):
+            a, b = J[h]
+            src = raw[h].rearrange("p (j l t) -> p l t j", j=b - a, t=PACK)
+            nc.scalar.copy(w_bf01[g][:, :, :, a:b], src[:, :, :2])
+            nc.gpsimd.tensor_copy(w_bf23[g][:].rearrange("p t l j -> p l t j")[:, :, :, a:b], src[:, :, 2:])
 
-        def quantise_w(planes, rounded):
-            width = len(planes) * P
-            words = keep.tile([P, width], U32, name=f"w_words{planes[0]}", align_bytes=64)
-            scale = keep.tile([P, width], U8, name=f"w_scales{planes[0]}", align_bytes=64)
-            nc.vector.quantize_mx(out=words[:].bitcast(FP8X4), scales=scale[:], in_=rounded)
-            for i, t in enumerate(planes):
-                w_words[t], w_scales[t] = words[:, i * P : (i + 1) * P], scale[:, i * P : (i + 1) * P]
+        for h in range(2):
+            round_w(w_lo, 0, h)
 
-        def project(t, lo, hi, bank):
-            acc = psum.tile([P, hi - lo], F32, name=f"acc{t}_{lo}", tag=bank)
+        words = {i: keep.tile([P, P], U32, name=f"w_words{i}", align_bytes=64)[:] for i in range(2)}
+        wscale = {i: keep.tile([P, P], U8, name=f"w_scales{i}", align_bytes=64)[:] for i in range(PACK)}
+
+        def quantise_w(i, a, b, rounded):
+            nc.vector.quantize_mx(out=words[i][:, a:b].bitcast(FP8X4), scales=wscale[i][:, a:b], in_=rounded)
+
+        def project(i, a, b, acc):
             nc.tensor.matmul_mx(
-                out=acc[:],
-                lhsT=w_words[t].bitcast(FP8X4),
-                lhsT_scale=w_scales[t],
-                rhs=xw[:, lo:hi].bitcast(FP8X4),
-                rhs_scale=xs[:, lo:hi],
+                out=acc,
+                lhsT=words[i].bitcast(FP8X4),
+                lhsT_scale=wscale[i],
+                rhs=xw[:, a:b].bitcast(FP8X4),
+                rhs_scale=xs[:, a:b],
                 start=True,
                 stop=True,
             )
-            nc.scalar.copy(y[t][:, lo:hi], acc[:])
 
-        def scatter(t, lo, hi):
-            nc.vector.tensor_copy(plane[t][:].indirect(slot_sb[:, lo // STRIPE : hi // STRIPE]), y[t][:, lo:hi])
+        def scatter(i, a, b, values):
+            nc.vector.tensor_copy(win[i][:].indirect(slot_sb[:, a // STRIPE : b // STRIPE]), values)
 
-        for t in (first, second, third):
-            y[t] = keep.tile([P, S], F32, name=f"y{t}", tag=f"y{t}", align_bytes=64)
-        quantise_w((2,), w_bf[:, 0, 1].rearrange("p m j -> p (m j)"))
-        quantise_w((0,), w_bf[:, 0, 0].rearrange("p m j -> p (m j)"))
-        for lo, hi in PIECES:
-            nc.vector.tensor_copy(xw[:, lo:hi], xw_all[:].indirect(offs_sb[:, lo // STRIPE : hi // STRIPE]))
-            if hi == LEAD:
-                project(first, lo, hi, bank="lead")
-            project(second, lo, hi, bank=f"second{lo}")
+        quantise_w(0, 0, P, w_bf01[0][:].rearrange("p l t j -> p (l t j)"))
+        y_lead = keep.tile([P, LEAD], F32, name="y_lead", align_bytes=64)
+        acc_rest = psum.tile([P, REST], F32, name="acc_rest")
+        for a, b in PIECES:
+            nc.vector.tensor_copy(xw[:, a:b], xw_all[:].indirect(offs_sb[:, a // STRIPE : b // STRIPE]))
+            if b <= LEAD:
+                acc = psum.tile([P, b - a], F32, name=f"acc_lead{a}")
+                project(0, a, b, acc[:])
+                nc.scalar.copy(y_lead[:, a:b], acc[:])
+            else:
+                project(0, a, b, acc_rest[:])
+        words23 = keep.tile([P, 2 * P], U32, name="w_words23", tag="xw_all", align_bytes=64)
+        words[2], words[3] = words23[:, :P], words23[:, P:]
+        for t in range(2):
+            quantise_w(2 + t, 0, HALF, w_bf23[0][:, t].rearrange("p l j -> p (l j)"))
 
+        scatter(0, 0, LEAD, y_lead[:])
+        early, late = (w_hi[h].rearrange("p (j l t) -> p l t j", j=2, t=PACK) for h in range(2))
+        hi23 = w_bf23[1][:].rearrange("p t l j -> p l t j")
+        nc.gpsimd.tensor_copy(w_bf01[1][:, :, :, :2], early[:, :, :2])
+        nc.gpsimd.tensor_copy(hi23[:, :, :, :2], early[:, :, 2:])
+        nc.scalar.copy(w_bf01[1][:, :, :, 2:], late[:, :, :2])
+        nc.scalar.copy(hi23[:, :, :, 2:], late[:, :, 2:])
+        quantise_w(1, 0, P, w_bf01[1][:].rearrange("p l t j -> p (l t j)"))
+        for t in range(2):
+            quantise_w(2 + t, HALF, P, w_bf23[1][:, t].rearrange("p l j -> p (l j)"))
+        y_rest = keep.tile([P, REST], F32, name="y_rest", tag="late", align_bytes=64)
+        nc.scalar.copy(y_rest[:], acc_rest[:])
+        scatter(0, LEAD, S, y_rest[:])
+
+        y = {}
+        for i in range(1, PACK):
+            acc = psum.tile([P, S], F32, name=f"acc{i}")
+            project(i, 0, S, acc[:])
+            y[i] = keep.tile([P, S], F32, name=f"y{i}", align_bytes=64)
+            nc.scalar.copy(y[i][:], acc[:])
+
+        MOVES = ((0, 2 * GROUP), (2 * GROUP, U))
+        moved = [keep.tile([P, 2, b - a], F32, name=f"moved{a}", align_bytes=64) for a, b in MOVES]
         out_bf = keep.tile([P, U, PACK], BF16, name="out_bf", align_bytes=64)
         codes = keep.tile([P, U], U32, name="codes", align_bytes=64)
         scales = keep.tile([P, U], U8, name="scales", align_bytes=64)
 
-        scatter(first, 0, LEAD)
-        scatter(second, 0, S)
-        quantise_w((1, 3), w_bf[:, 1].rearrange("p a m j -> p (a m j)"))
-        project(third, 0, S, bank="shared")
-        for lo, hi in PIECES[1:]:
-            project(first, lo, hi, bank="shared")
-        nc.sync.dma_start(out_rows[:, second, :], plane[second][:])
-        nc.scalar.copy(out_bf[:, :, second], plane[second][:])
+        def move(i):
+            for h, (a, b) in enumerate(MOVES):
+                for t in range(2):
+                    nc.sync.dma_start(moved[h][i * HALF : (i + 1) * HALF, t, :], win[i][t:P:2, a:b])
+            nc.sync.dma_start(rows_of(out_rows, i), win[i][:])
 
-        y[last] = keep.tile([P, S], F32, name=f"y{last}", tag=f"y{second}", align_bytes=64)
-        project(last, 0, S, bank="last")
+        def gp_round(dst, src):
+            nc.gpsimd.tensor_copy(dst, src)
 
-        for t, lo in ((first, LEAD), (third, 0)):
-            scatter(t, lo, S)
-            nc.sync.dma_start(out_rows[:, t, :], plane[t][:])
-            nc.scalar.copy(out_bf[:, :SCALAR_COLS, t], plane[t][:, :SCALAR_COLS])
-            nc.gpsimd.tensor_copy(out_bf[:, SCALAR_COLS:, t], plane[t][:, SCALAR_COLS:])
+        move(0)
+        scatter(1, 0, S, y[1][:])
+        move(1)
+        groups_bf = out_bf[:].rearrange("p (g c) t -> p g c t", c=GROUP)
+        upper = moved[1][:].rearrange("p t (g c) -> p g c t", c=GROUP)
+        nc.scalar.copy(out_bf[:, : 2 * GROUP, 0:2], moved[0][:].rearrange("p t c -> p c t"))
+        nc.scalar.copy(groups_bf[:, 4:, GROUP - PARK :, 2:4], upper[:, 2:, GROUP - PARK :])
+        nc.scalar.copy(groups_bf[:, 2:4, :, 0:2], upper[:, :2])
+        nc.scalar.copy(groups_bf[:, 4:, : GROUP - PARK, 0:2], upper[:, 2:, : GROUP - PARK])
+        nc.scalar.copy(groups_bf[:, 4:, GROUP - PARK :, 0:2], groups_bf[:, 4:, GROUP - PARK :, 2:4])
 
-        scatter(last, 0, S)
-        nc.sync.dma_start(out_rows[:, last, :], plane[last][:])
-        for lo, hi in ROUNDED:
-            copy = nc.vector.tensor_copy if lo < VECTOR_COLS else nc.scalar.copy
-            copy(out_bf[:, lo:hi, last], plane[last][:, lo:hi])
+        scatter(2, 0, S, y[2][:])
+        nc.sync.dma_start(rows_of(out_rows, 2), win[2][:])
+        groups = win[2][:].rearrange("p (g c) -> p g c", c=GROUP)
+        gp_round(groups_bf[:, :, :PARK, 3], groups[:, :, :PARK])
+        gp_round(groups_bf[:, :4, PARK:, 2], groups[:, :4, PARK:])
+        gp_round(groups_bf[:, 4:, PARK:GP_COLS, 2], groups[:, 4:, PARK:GP_COLS])
+        gp_round(groups_bf[:, :, :PARK, 2], groups_bf[:, :, :PARK, 3])
+        nc.scalar.copy(groups_bf[:, 4:, GP_COLS:, 2], groups[:, 4:, GP_COLS:])
+
+        scatter(3, 0, S, y[3][:])
+        nc.sync.dma_start(rows_of(out_rows, 3), win[3][:])
+        for a, b in ROUNDED:
+            copy = nc.vector.tensor_copy if a < VECTOR_COLS else nc.scalar.copy
+            copy(out_bf[:, a:b, 3], win[3][:, a:b])
 
         stored = 0
-        for lo, hi in QUANTISED:
+        for a, b in QUANTISED:
             nc.vector.quantize_mx(
-                out=codes[:, lo:hi].bitcast(FP8X4),
-                scales=scales[:, lo:hi],
-                in_=out_bf[:, lo:hi, :].rearrange("p c t -> p (c t)"),
+                out=codes[:, a:b].bitcast(FP8X4),
+                scales=scales[:, a:b],
+                in_=out_bf[:, a:b, :].rearrange("p c t -> p (c t)"),
             )
-            if hi in STORE_ENDS:
-                nc.sync.dma_start(out_words[:, stored:hi], codes[:, stored:hi].bitcast(I32))
-                stored = hi
+            if b in STORE_ENDS:
+                nc.sync.dma_start(out_words[:, stored:b], codes[:, stored:b].bitcast(I32))
+                stored = b
         for r in range(PACK):
             queue = nc.scalar if r % 2 == 0 else nc.sync
             queue.dma_start(out_2[0][r:SCALE_ROWS:PACK, :].bitcast(I32), scales[r:P:QUADRANT, :].bitcast(I32))

@@ -1,6 +1,7 @@
 from contextlib import ExitStack
 
 import concourse.mybir as mybir
+from concourse.masks import make_identity
 
 K, T, S, N, U = 512, 1024, 512, 512, 1024
 FLOPS = 2 * K * N * S
@@ -83,6 +84,9 @@ def tile_picked_kvput_none_po_kernel(
         for i in range(1, PACK):
             nc.sync.dma_start(win[i][:], rows_of(mem_rows, i))
 
+        identity = keep.tile([P, P], F32, name="identity", align_bytes=64)
+        make_identity(nc, identity[:])
+
         xs = keep.tile([P, S], U8, name="xs", align_bytes=64)
         xw = keep.tile([P, S], U32, name="xw", align_bytes=64)
         nc.vector.tensor_copy(xs[:], xs_all[:].indirect(offs_sb[:]))
@@ -125,7 +129,7 @@ def tile_picked_kvput_none_po_kernel(
         for a, b in PIECES:
             nc.vector.tensor_copy(xw[:, a:b], xw_all[:].indirect(offs_sb[:, a // STRIPE : b // STRIPE]))
             if b <= LEAD:
-                acc = psum.tile([P, b - a], F32, name=f"acc_lead{a}")
+                acc = psum.tile([P, b - a], F32, name=f"acc_lead{a}", tag=f"turn{a // P}")
                 project(0, a, b, acc[:])
                 nc.scalar.copy(y_lead[:, a:b], acc[:])
             else:
@@ -151,22 +155,24 @@ def tile_picked_kvput_none_po_kernel(
 
         y = {}
         for i in range(1, PACK):
-            acc = psum.tile([P, S], F32, name=f"acc{i}")
+            acc = psum.tile([P, S], F32, name=f"acc{i}", tag=f"acc{i}")
             project(i, 0, S, acc[:])
             y[i] = keep.tile([P, S], F32, name=f"y{i}", align_bytes=64)
             nc.scalar.copy(y[i][:], acc[:])
 
-        MOVES = ((0, 2 * GROUP), (2 * GROUP, U))
-        moved = [keep.tile([P, 2, b - a], F32, name=f"moved{a}", align_bytes=64) for a, b in MOVES]
+        turned = [keep.tile([P, 4, 2 * P], BF16, name=f"turned{h}", align_bytes=64) for h in range(2)]
         out_bf = keep.tile([P, U, PACK], BF16, name="out_bf", align_bytes=64)
         codes = keep.tile([P, U], U32, name="codes", align_bytes=64)
         scales = keep.tile([P, U], U8, name="scales", align_bytes=64)
 
         def move(i):
-            for h, (a, b) in enumerate(MOVES):
-                for t in range(2):
-                    nc.sync.dma_start(moved[h][i * HALF : (i + 1) * HALF, t, :], win[i][t:P:2, a:b])
             nc.sync.dma_start(rows_of(out_rows, i), win[i][:])
+            for h in range(2):
+                bank = psum.tile([P, 4, P], F32, name=f"turn{i}_{h}", tag=f"turn{h}")
+                for g in range(4):
+                    c = (4 * h + g) * GROUP
+                    nc.tensor.transpose(bank[:, g, :], win[i][:, c : c + GROUP], identity[:])
+                nc.scalar.copy(turned[h][:, :, i * P : (i + 1) * P], bank[:])
 
         def gp_round(dst, src):
             nc.gpsimd.tensor_copy(dst, src)
@@ -175,11 +181,15 @@ def tile_picked_kvput_none_po_kernel(
         scatter(1, 0, S, y[1][:])
         move(1)
         groups_bf = out_bf[:].rearrange("p (g c) t -> p g c t", c=GROUP)
-        upper = moved[1][:].rearrange("p t (g c) -> p g c t", c=GROUP)
-        nc.scalar.copy(out_bf[:, : 2 * GROUP, 0:2], moved[0][:].rearrange("p t c -> p c t"))
-        nc.scalar.copy(groups_bf[:, 4:, GROUP - PARK :, 2:4], upper[:, 2:, GROUP - PARK :])
-        nc.scalar.copy(groups_bf[:, 2:4, :, 0:2], upper[:, :2])
-        nc.scalar.copy(groups_bf[:, 4:, : GROUP - PARK, 0:2], upper[:, 2:, : GROUP - PARK])
+        back = []
+        for h in range(2):
+            bank = psum.tile([P, 4, P], F32, name=f"back{h}", tag=f"acc{1 + h}")
+            for g in range(4):
+                nc.tensor.transpose(bank[:, g, :], turned[h][:, g, :].bitcast(F32), identity[:])
+            back.append(bank[:].rearrange("p g c -> p (g c)").bitcast(BF16).rearrange("p (g c t) -> p g c t", g=4, t=2))
+        nc.scalar.copy(groups_bf[:, :4, :, 0:2], back[0])
+        nc.scalar.copy(groups_bf[:, 4:, GROUP - PARK :, 2:4], back[1][:, :, GROUP - PARK :])
+        nc.scalar.copy(groups_bf[:, 4:, : GROUP - PARK, 0:2], back[1][:, :, : GROUP - PARK])
         nc.scalar.copy(groups_bf[:, 4:, GROUP - PARK :, 0:2], groups_bf[:, 4:, GROUP - PARK :, 2:4])
 
         scatter(2, 0, S, y[2][:])

@@ -29,7 +29,7 @@ EARLY_J = 3
 VECTOR_COLS = 512
 PARK = 4
 GROUP = 128
-GP_COLS = 88
+GP_END = 816
 ROUNDED = ((0, 256), (256, 512), (512, 768), (768, 896), (896, 1024))
 QUANTISED = ((0, 256), (256, 384), (384, 512), (512, 768), (768, 896), (896, 1024))
 STORE_ENDS = (384, 768, 1024)
@@ -125,7 +125,7 @@ def tile_picked_kvput_none_po_kernel(
 
         quantise_w(0, 0, P, w_bf01[0][:].rearrange("p l t j -> p (l t j)"))
         y_lead = keep.tile([P, LEAD], F32, name="y_lead", align_bytes=64)
-        acc_rest = psum.tile([P, REST], F32, name="acc_rest")
+        acc_rest = psum.tile([P, REST], F32, name="acc_rest", tag="acc0")
         for a, b in PIECES:
             nc.vector.tensor_copy(xw[:, a:b], xw_all[:].indirect(offs_sb[:, a // STRIPE : b // STRIPE]))
             if b <= LEAD:
@@ -160,17 +160,17 @@ def tile_picked_kvput_none_po_kernel(
             y[i] = keep.tile([P, S], F32, name=f"y{i}", align_bytes=64)
             nc.scalar.copy(y[i][:], acc[:])
 
-        turned = [keep.tile([P, 4, 2 * P], BF16, name=f"turned{h}", align_bytes=64) for h in range(2)]
+        turned = [keep.tile([P, 2, 2 * P], BF16, name=f"turned{h}", align_bytes=64) for h in range(4)]
         out_bf = keep.tile([P, U, PACK], BF16, name="out_bf", align_bytes=64)
         codes = keep.tile([P, U], U32, name="codes", align_bytes=64)
         scales = keep.tile([P, U], U8, name="scales", align_bytes=64)
 
         def move(i):
             nc.sync.dma_start(rows_of(out_rows, i), win[i][:])
-            for h in range(2):
-                bank = psum.tile([P, 4, P], F32, name=f"turn{i}_{h}", tag=f"turn{h}")
-                for g in range(4):
-                    c = (4 * h + g) * GROUP
+            for h in range(4):
+                bank = psum.tile([P, 2, P], F32, name=f"turn{i}_{h}", tag=f"turn{h}")
+                for g in range(2):
+                    c = (2 * h + g) * GROUP
                     nc.tensor.transpose(bank[:, g, :], win[i][:, c : c + GROUP], identity[:])
                 nc.scalar.copy(turned[h][:, :, i * P : (i + 1) * P], bank[:])
 
@@ -180,26 +180,29 @@ def tile_picked_kvput_none_po_kernel(
         move(0)
         scatter(1, 0, S, y[1][:])
         move(1)
-        groups_bf = out_bf[:].rearrange("p (g c) t -> p g c t", c=GROUP)
         back = []
-        for h in range(2):
-            bank = psum.tile([P, 4, P], F32, name=f"back{h}", tag=f"acc{1 + h}")
-            for g in range(4):
+        for h in range(4):
+            bank = psum.tile([P, 2, P], F32, name=f"back{h}", tag=f"acc{h}")
+            for g in range(2):
                 nc.tensor.transpose(bank[:, g, :], turned[h][:, g, :].bitcast(F32), identity[:])
-            back.append(bank[:].rearrange("p g c -> p (g c)").bitcast(BF16).rearrange("p (g c t) -> p g c t", g=4, t=2))
-        nc.scalar.copy(groups_bf[:, :4, :, 0:2], back[0])
-        nc.scalar.copy(groups_bf[:, 4:, GROUP - PARK :, 2:4], back[1][:, :, GROUP - PARK :])
-        nc.scalar.copy(groups_bf[:, 4:, : GROUP - PARK, 0:2], back[1][:, :, : GROUP - PARK])
-        nc.scalar.copy(groups_bf[:, 4:, GROUP - PARK :, 0:2], groups_bf[:, 4:, GROUP - PARK :, 2:4])
+            back.append(bank[:].rearrange("p g c -> p (g c)").bitcast(BF16).rearrange("p (c t) -> p c t", t=2))
+        STAGE = 2 * GROUP
+        for h in range(2):
+            nc.scalar.copy(out_bf[:, h * STAGE : (h + 1) * STAGE, 0:2], back[h])
+        nc.scalar.copy(out_bf[:, U - PARK :, 2:4], back[3][:, STAGE - PARK :])
+        nc.scalar.copy(out_bf[:, 2 * STAGE : 3 * STAGE, 0:2], back[2])
+        nc.scalar.copy(out_bf[:, U - PARK :, 0:2], out_bf[:, U - PARK :, 2:4])
+        nc.scalar.copy(out_bf[:, 3 * STAGE : U - PARK, 0:2], back[3][:, : STAGE - PARK])
 
         scatter(2, 0, S, y[2][:])
         nc.sync.dma_start(rows_of(out_rows, 2), win[2][:])
-        groups = win[2][:].rearrange("p (g c) -> p g c", c=GROUP)
-        gp_round(groups_bf[:, :, :PARK, 3], groups[:, :, :PARK])
-        gp_round(groups_bf[:, :4, PARK:, 2], groups[:, :4, PARK:])
-        gp_round(groups_bf[:, 4:, PARK:GP_COLS, 2], groups[:, 4:, PARK:GP_COLS])
-        gp_round(groups_bf[:, :, :PARK, 2], groups_bf[:, :, :PARK, 3])
-        nc.scalar.copy(groups_bf[:, 4:, GP_COLS:, 2], groups[:, 4:, GP_COLS:])
+        stages_bf = out_bf[:].rearrange("p (g c) t -> p g c t", c=STAGE)
+        stages = win[2][:].rearrange("p (g c) -> p g c", c=STAGE)
+        gp_round(stages_bf[:, :, :PARK, 3], stages[:, :, :PARK])
+        gp_round(stages_bf[:, :3, PARK:, 2], stages[:, :3, PARK:])
+        gp_round(out_bf[:, 3 * STAGE + PARK : GP_END, 2], win[2][:, 3 * STAGE + PARK : GP_END])
+        gp_round(stages_bf[:, :, :PARK, 2], stages_bf[:, :, :PARK, 3])
+        nc.scalar.copy(out_bf[:, GP_END:, 2], win[2][:, GP_END:])
 
         scatter(3, 0, S, y[3][:])
         nc.sync.dma_start(rows_of(out_rows, 3), win[3][:])

@@ -29,7 +29,6 @@ EARLY_J = 3
 VECTOR_COLS = 512
 PARK = 4
 GROUP = 128
-GP_END = 816
 ROUNDED = ((0, 256), (256, 512), (512, 768), (768, 896), (896, 1024))
 QUANTISED = ((0, 256), (256, 384), (384, 512), (512, 768), (768, 896), (896, 1024))
 STORE_ENDS = (384, 768, 1024)
@@ -198,11 +197,10 @@ def tile_picked_kvput_none_po_kernel(
         nc.sync.dma_start(rows_of(out_rows, 2), win[2][:])
         stages_bf = out_bf[:].rearrange("p (g c) t -> p g c t", c=STAGE)
         stages = win[2][:].rearrange("p (g c) -> p g c", c=STAGE)
-        gp_round(stages_bf[:, :, :PARK, 3], stages[:, :, :PARK])
+        gp_round(stages_bf[:, :3, :PARK, 3], stages[:, :3, :PARK])
         gp_round(stages_bf[:, :3, PARK:, 2], stages[:, :3, PARK:])
-        gp_round(out_bf[:, 3 * STAGE + PARK : GP_END, 2], win[2][:, 3 * STAGE + PARK : GP_END])
-        gp_round(stages_bf[:, :, :PARK, 2], stages_bf[:, :, :PARK, 3])
-        nc.scalar.copy(out_bf[:, GP_END:, 2], win[2][:, GP_END:])
+        gp_round(stages_bf[:, :3, :PARK, 2], stages_bf[:, :3, :PARK, 3])
+        nc.scalar.copy(stages_bf[:, 3, :, 2], stages[:, 3])
 
         scatter(3, 0, S, y[3][:])
         nc.sync.dma_start(rows_of(out_rows, 3), win[3][:])

@@ -28,6 +28,7 @@ PIECES = ((0, 128), (128, 256), (256, 512))
 EARLY_J = 3
 VECTOR_COLS = 512
 PARK = 4
+HELD = 16
 GROUP = 128
 ROUNDED = ((0, 256), (256, 512), (512, 768), (768, 896), (896, 1024))
 QUANTISED = ((0, 256), (256, 384), (384, 512), (512, 768), (768, 896), (896, 1024))
@@ -60,8 +61,9 @@ def tile_picked_kvput_none_po_kernel(
         xw_all = keep.tile([P, T], U32, name="xw_all", tag="xw_all", align_bytes=64)
         w_lo = [keep.tile([P, (b - a) * HN], F32, name=f"w_lo{a}", align_bytes=64)[:] for a, b in J]
         w_hi_early = keep.tile([P, 2 * HN], F32, name="w_hi_early", align_bytes=64)
-        w_hi_late = keep.tile([P, 2 * HN], F32, name="w_hi_late", tag="late", align_bytes=64)
-        w_hi = [w_hi_early[:], w_hi_late[:]]
+        shared = keep.tile([P, REST - HELD + 2 * HN], F32, name="shared", align_bytes=64)
+        y_rest = shared[:, :REST]
+        w_hi = [w_hi_early[:], shared[:, REST - HELD :]]
         win = [keep.tile([P, U], F32, name=f"win{i}", align_bytes=64) for i in range(PACK)]
 
         nc.vector.memset(xs_all[:].bitcast(I32), 0)
@@ -133,6 +135,7 @@ def tile_picked_kvput_none_po_kernel(
                 nc.scalar.copy(y_lead[:, a:b], acc[:])
             else:
                 project(0, a, b, acc_rest[:])
+                nc.scalar.copy(y_rest[:, : REST - HELD], acc_rest[:, : REST - HELD])
         words23 = keep.tile([P, 2 * P], U32, name="w_words23", tag="xw_all", align_bytes=64)
         words[2], words[3] = words23[:, :P], words23[:, P:]
         for t in range(2):
@@ -144,13 +147,13 @@ def tile_picked_kvput_none_po_kernel(
         nc.gpsimd.tensor_copy(w_bf01[1][:, :, :, :2], early[:, :, :2])
         nc.gpsimd.tensor_copy(hi23[:, :, :, :2], early[:, :, 2:])
         nc.scalar.copy(w_bf01[1][:, :, :, 2:], late[:, :, :2])
-        nc.scalar.copy(hi23[:, :, :, 2:], late[:, :, 2:])
+        nc.scalar.copy(hi23[:, : HELD // PACK, :, 2:], late[:, : HELD // PACK, 2:])
         quantise_w(1, 0, P, w_bf01[1][:].rearrange("p l t j -> p (l t j)"))
+        nc.scalar.copy(y_rest[:, REST - HELD :], acc_rest[:, REST - HELD :])
+        scatter(0, LEAD, S, y_rest)
+        nc.scalar.copy(hi23[:, HELD // PACK :, :, 2:], late[:, HELD // PACK :, 2:])
         for t in range(2):
             quantise_w(2 + t, HALF, P, w_bf23[1][:, t].rearrange("p l j -> p (l j)"))
-        y_rest = keep.tile([P, REST], F32, name="y_rest", tag="late", align_bytes=64)
-        nc.scalar.copy(y_rest[:], acc_rest[:])
-        scatter(0, LEAD, S, y_rest[:])
 
         y = {}
         for i in range(1, PACK):

@@ -72,8 +72,8 @@ def tile_picked_kvput_none_po_kernel(
             a, b = cut[h]
             nc.sync.dma_start(dst[h].rearrange("p (j n) -> p j n", j=b - a), w_rows[:, a:b, cols])
 
-        load_w(w_lo, 0, slice(0, HN), J)
         nc.sync.dma_start(offs_sb[:], offs)
+        load_w(w_lo, 0, slice(0, HN), J)
         for r in range(PACK):
             nc.sync.dma_start(xs_all[r:P:QUADRANT, :].bitcast(I32), x_scales[0][r:SCALE_ROWS:PACK, :].bitcast(I32))
         load_w(w_lo, 1, slice(0, HN), J)

@@ -1,7 +1,6 @@
 from contextlib import ExitStack
 
 import concourse.mybir as mybir
-from concourse.masks import make_identity
 
 K, T, S, N, U = 512, 1024, 512, 512, 1024
 FLOPS = 2 * K * N * S
@@ -13,26 +12,26 @@ U32 = mybir.dt.uint32
 U16 = mybir.dt.uint16
 U8 = mybir.dt.uint8
 FP8X4 = mybir.dt.float8_e4m3fn_x4
-MULT = mybir.AluOpType.mult
-ADD = mybir.AluOpType.add
+COPY = mybir.ActivationFunctionType.Copy
 
 P = 128
-HALF = 64
 PACK = 4
 STRIPE = 16
 QUADRANT = 32
 SCALE_ROWS = 16
 
+HALF_N = N // 2
+QUADS = HALF_N // PACK
 LEAD = 256
-PIECES = ((0, 128), (128, 256), (256, 512))
-EARLY_J = 3
-VECTOR_COLS = 512
-PARK = 4
-HELD = 16
-GROUP = 128
-ROUNDED = ((0, 256), (256, 512), (512, 768), (768, 896), (896, 1024))
-QUANTISED = ((0, 256), (256, 384), (384, 512), (512, 768), (768, 896), (896, 1024))
-STORE_ENDS = (384, 768, 1024)
+GATHERED = ((0, 128), (128, 256), (256, 512))
+VECTOR_COLS = 640
+PAIRED = ((0, 256), (256, 512), (512, 768), (768, 1024))
+VECTOR_TAIL = ((0, 256), (256, 640))
+SCALAR_TAIL = ((640, 832), (832, 1024))
+WOVEN_VECTOR = ((0, 256), (256, 512))
+WOVEN_SCALAR = ((640, 768), (512, 640), (768, 1024))
+QUANTISED = ((0, 256), (256, 512), (512, 768), (768, 1024))
+STORE_ENDS = (256, 768, 1024)
 
 
 def tile_picked_kvput_none_po_kernel(
@@ -43,13 +42,6 @@ def tile_picked_kvput_none_po_kernel(
     out_rows = out_0.rearrange("(p t) c -> p t c", t=PACK)
     w_rows = w1.rearrange("(p j) n -> p j n", j=PACK)
     out_words = out_1[0].rearrange("p c r -> p (c r)").bitcast(I32)
-    HN = N // 2
-    REST = S - LEAD
-    J = ((0, EARLY_J), (EARLY_J, PACK))
-    JH = ((0, 2), (2, PACK))
-
-    def rows_of(ap, i):
-        return ap[i * HALF : (i + 1) * HALF, 0:2, :] if i < 2 else ap[:, i, :]
 
     with ExitStack() as ctx:
         keep = ctx.enter_context(tc.tile_pool(name="keep", bufs=1))
@@ -59,157 +51,123 @@ def tile_picked_kvput_none_po_kernel(
         slot_sb = keep.tile([P, S // STRIPE], U16, name="slot_sb")
         xs_all = keep.tile([P, T], U8, name="xs_all", align_bytes=64)
         xw_all = keep.tile([P, T], U32, name="xw_all", tag="xw_all", align_bytes=64)
-        w_lo = [keep.tile([P, (b - a) * HN], F32, name=f"w_lo{a}", align_bytes=64)[:] for a, b in J]
-        w_hi_early = keep.tile([P, 2 * HN], F32, name="w_hi_early", align_bytes=64)
-        shared = keep.tile([P, REST - HELD + 2 * HN], F32, name="shared", align_bytes=64)
-        y_rest = shared[:, :REST]
-        w_hi = [w_hi_early[:], shared[:, REST - HELD :]]
-        win = [keep.tile([P, U], F32, name=f"win{i}", align_bytes=64) for i in range(PACK)]
+        w_raw = [keep.tile([P, PACK, HALF_N], F32, name=f"w_raw{h}", align_bytes=64) for h in range(2)]
+        win = [keep.tile([P, U], F32, name=f"win{t}", align_bytes=64) for t in range(PACK)]
 
         nc.vector.memset(xs_all[:].bitcast(I32), 0)
 
-        def load_w(dst, h, cols, cut):
-            a, b = cut[h]
-            nc.sync.dma_start(dst[h].rearrange("p (j n) -> p j n", j=b - a), w_rows[:, a:b, cols])
-
         nc.sync.dma_start(offs_sb[:], offs)
-        load_w(w_lo, 0, slice(0, HN), J)
+        nc.sync.dma_start(w_raw[0][:], w_rows[:, :, :HALF_N])
         for r in range(PACK):
             nc.sync.dma_start(xs_all[r:P:QUADRANT, :].bitcast(I32), x_scales[0][r:SCALE_ROWS:PACK, :].bitcast(I32))
-        load_w(w_lo, 1, slice(0, HN), J)
+        nc.sync.dma_start(w_raw[1][:], w_rows[:, :, HALF_N:])
         nc.sync.dma_start(xw_all[:].bitcast(I32), x_words[0].rearrange("p c r -> p (c r)").bitcast(I32))
-        nc.sync.dma_start(win[0][:], rows_of(mem_rows, 0))
+        nc.sync.dma_start(win[0][:], mem_rows[:, 0, :])
         nc.sync.dma_start(slot_sb[:], slot)
-        load_w(w_hi, 0, slice(HN, N), JH)
-        load_w(w_hi, 1, slice(HN, N), JH)
-        for i in range(1, PACK):
-            nc.sync.dma_start(win[i][:], rows_of(mem_rows, i))
-
-        identity = keep.tile([P, P], F32, name="identity", align_bytes=64)
-        make_identity(nc, identity[:])
+        for t in (1, 3, 2):
+            nc.sync.dma_start(win[t][:], mem_rows[:, t, :])
 
         xs = keep.tile([P, S], U8, name="xs", align_bytes=64)
-        xw = keep.tile([P, S], U32, name="xw", align_bytes=64)
         nc.vector.tensor_copy(xs[:], xs_all[:].indirect(offs_sb[:]))
 
-        w_bf01 = [keep.tile([P, HALF, 2, PACK], BF16, name=f"w_bf{i}", align_bytes=64) for i in range(2)]
-        w_bf23 = [keep.tile([P, 2, HALF, PACK], BF16, name=f"w_bf23_{g}", align_bytes=64) for g in range(2)]
+        w_bf = [keep.tile([P, 2, P, PACK], BF16, name=f"w_bf{u}", tag=f"w_bf{u}", align_bytes=64) for u in range(2)]
 
-        def round_w(raw, g, h):
-            a, b = J[h]
-            src = raw[h].rearrange("p (j l t) -> p l t j", j=b - a, t=PACK)
-            nc.scalar.copy(w_bf01[g][:, :, :, a:b], src[:, :, :2])
-            nc.gpsimd.tensor_copy(w_bf23[g][:].rearrange("p t l j -> p l t j")[:, :, :, a:b], src[:, :, 2:])
+        def w_share(h, u):
+            src = w_raw[h][:].rearrange("p j (l t) -> p l t j", t=PACK)
+            dst = w_bf[u][:].rearrange("p e l j -> p l e j")
+            return dst[:, h * QUADS : (h + 1) * QUADS], src[:, :, 2 * u : 2 * u + 2]
 
-        for h in range(2):
-            round_w(w_lo, 0, h)
+        w_words = {t: keep.tile([P, P], U32, name=f"w_words{t}", align_bytes=64)[:] for t in range(2)}
+        w_scales = [keep.tile([P, P], U8, name=f"w_scales{t}", align_bytes=64) for t in range(PACK)]
 
-        words = {i: keep.tile([P, P], U32, name=f"w_words{i}", align_bytes=64)[:] for i in range(2)}
-        wscale = {i: keep.tile([P, P], U8, name=f"w_scales{i}", align_bytes=64)[:] for i in range(PACK)}
+        def quantise_w(t):
+            nc.vector.quantize_mx(
+                out=w_words[t].bitcast(FP8X4),
+                scales=w_scales[t][:],
+                in_=w_bf[t // 2][:, t % 2].rearrange("p l j -> p (l j)"),
+            )
 
-        def quantise_w(i, a, b, rounded):
-            nc.vector.quantize_mx(out=words[i][:, a:b].bitcast(FP8X4), scales=wscale[i][:, a:b], in_=rounded)
+        nc.scalar.activation(*w_share(0, 0), COPY)
+        nc.gpsimd.tensor_copy(*w_share(0, 1))
+        nc.scalar.copy(*w_share(1, 0))
+        nc.gpsimd.tensor_copy(*w_share(1, 1))
+        quantise_w(0)
+        quantise_w(1)
+        xw = keep.tile([P, S], U32, name="xw", tag="w_bf0", align_bytes=64)
 
-        def project(i, a, b, acc):
+        def project(t, a, b, acc):
             nc.tensor.matmul_mx(
                 out=acc,
-                lhsT=words[i].bitcast(FP8X4),
-                lhsT_scale=wscale[i],
+                lhsT=w_words[t].bitcast(FP8X4),
+                lhsT_scale=w_scales[t][:],
                 rhs=xw[:, a:b].bitcast(FP8X4),
                 rhs_scale=xs[:, a:b],
                 start=True,
                 stop=True,
             )
 
-        def scatter(i, a, b, values):
-            nc.vector.tensor_copy(win[i][:].indirect(slot_sb[:, a // STRIPE : b // STRIPE]), values)
+        def target(t, a, b):
+            return win[t][:].indirect(slot_sb[:, a // STRIPE : b // STRIPE])
 
-        quantise_w(0, 0, P, w_bf01[0][:].rearrange("p l t j -> p (l t j)"))
-        y_lead = keep.tile([P, LEAD], F32, name="y_lead", align_bytes=64)
-        acc_rest = psum.tile([P, REST], F32, name="acc_rest", tag="acc0")
-        for a, b in PIECES:
+        pair_words = keep.tile([P, 2 * U], F32, name="pair_words", align_bytes=64)
+        y = {t: keep.tile([P, S], F32, name=f"y{t}", align_bytes=64)[:] for t in range(2)}
+        y[3], y[2] = pair_words[:, U : U + S], pair_words[:, U + S :]
+        for a, b in GATHERED:
             nc.vector.tensor_copy(xw[:, a:b], xw_all[:].indirect(offs_sb[:, a // STRIPE : b // STRIPE]))
             if b <= LEAD:
-                acc = psum.tile([P, b - a], F32, name=f"acc_lead{a}", tag=f"turn{a // P}")
-                project(0, a, b, acc[:])
-                nc.scalar.copy(y_lead[:, a:b], acc[:])
-            else:
-                project(0, a, b, acc_rest[:])
-                nc.scalar.copy(y_rest[:, : REST - HELD], acc_rest[:, : REST - HELD])
-        words23 = keep.tile([P, 2 * P], U32, name="w_words23", tag="xw_all", align_bytes=64)
-        words[2], words[3] = words23[:, :P], words23[:, P:]
-        for t in range(2):
-            quantise_w(2 + t, 0, HALF, w_bf23[0][:, t].rearrange("p l j -> p (l j)"))
+                lead = psum.tile([P, b - a], F32, name=f"lead{a}", tag=f"lead{a}")
+                project(0, a, b, lead[:])
+                nc.scalar.copy(y[0][:, a:b], lead[:])
+        late_words = keep.tile([P, 2 * P], U32, name="late_words", tag="xw_all", align_bytes=64)
+        w_words[2], w_words[3] = late_words[:, :P], late_words[:, P:]
+        quantise_w(3)
+        quantise_w(2)
 
-        scatter(0, 0, LEAD, y_lead[:])
-        early, late = (w_hi[h].rearrange("p (j l t) -> p l t j", j=2, t=PACK) for h in range(2))
-        hi23 = w_bf23[1][:].rearrange("p t l j -> p l t j")
-        nc.gpsimd.tensor_copy(w_bf01[1][:, :, :, :2], early[:, :, :2])
-        nc.gpsimd.tensor_copy(hi23[:, :, :, :2], early[:, :, 2:])
-        nc.scalar.copy(w_bf01[1][:, :, :, 2:], late[:, :, :2])
-        nc.scalar.copy(hi23[:, : HELD // PACK, :, 2:], late[:, : HELD // PACK, 2:])
-        quantise_w(1, 0, P, w_bf01[1][:].rearrange("p l t j -> p (l t j)"))
-        nc.scalar.copy(y_rest[:, REST - HELD :], acc_rest[:, REST - HELD :])
-        scatter(0, LEAD, S, y_rest)
-        nc.scalar.copy(hi23[:, HELD // PACK :, :, 2:], late[:, HELD // PACK :, 2:])
-        for t in range(2):
-            quantise_w(2 + t, HALF, P, w_bf23[1][:, t].rearrange("p l j -> p (l j)"))
+        def through(tag, copy, *pieces):
+            acc = psum.tile([P, len(pieces), LEAD], F32, name=f"acc{pieces[0][0]}_{pieces[0][1]}", tag=tag)
+            for i, (t, a) in enumerate(pieces):
+                project(t, a, a + LEAD, acc[:, i])
+            for i, (t, a) in enumerate(pieces):
+                copy(y[t][:, a : a + LEAD], acc[:, i])
 
-        y = {}
-        for i in range(1, PACK):
-            acc = psum.tile([P, S], F32, name=f"acc{i}", tag=f"acc{i}")
-            project(i, 0, S, acc[:])
-            y[i] = keep.tile([P, S], F32, name=f"y{i}", align_bytes=64)
-            nc.scalar.copy(y[i][:], acc[:])
+        nc.scalar.activation(target(0, 0, LEAD), y[0][:, :LEAD], COPY)
+        through("acc0", nc.vector.tensor_copy, (1, 0))
+        through("acc1", nc.vector.tensor_copy, (1, LEAD))
+        through("acc2", nc.vector.tensor_copy, (3, 0))
+        through("acc1", nc.scalar.copy, (0, LEAD), (3, LEAD))
+        through("acc2", nc.scalar.copy, (2, 0), (2, LEAD))
+        nc.vector.tensor_copy(target(1, 0, S), y[1])
+        nc.scalar.activation(target(0, LEAD, S), y[0][:, LEAD:], COPY)
+        nc.scalar.activation(target(2, 0, LEAD), y[2][:, :LEAD], COPY)
+        nc.scalar.activation(target(2, LEAD, S), y[2][:, LEAD:], COPY)
+        nc.vector.tensor_copy(target(3, 0, S), y[3])
+        for t in (0, 1, 3, 2):
+            nc.sync.dma_start(out_rows[:, t, :], win[t][:])
 
-        turned = [keep.tile([P, 2, 2 * P], BF16, name=f"turned{h}", align_bytes=64) for h in range(4)]
+        pairs = pair_words[:].bitcast(BF16).rearrange("p (u c e) -> p u c e", u=2, e=2)
         out_bf = keep.tile([P, U, PACK], BF16, name="out_bf", align_bytes=64)
         codes = keep.tile([P, U], U32, name="codes", align_bytes=64)
         scales = keep.tile([P, U], U8, name="scales", align_bytes=64)
 
-        def move(i):
-            nc.sync.dma_start(rows_of(out_rows, i), win[i][:])
-            for h in range(4):
-                bank = psum.tile([P, 2, P], F32, name=f"turn{i}_{h}", tag=f"turn{h}")
-                for g in range(2):
-                    c = (2 * h + g) * GROUP
-                    nc.tensor.transpose(bank[:, g, :], win[i][:, c : c + GROUP], identity[:])
-                nc.scalar.copy(turned[h][:, :, i * P : (i + 1) * P], bank[:])
+        def rounded(t, a, b):
+            return pairs[:, t // 2, a:b, t % 2], win[t][:, a:b]
 
-        def gp_round(dst, src):
-            nc.gpsimd.tensor_copy(dst, src)
+        woven = pair_words[:].rearrange("p (u c) -> p c u", u=2)
+        quad_words = out_bf[:].rearrange("p c t -> p (c t)").bitcast(F32).rearrange("p (c u) -> p c u", u=2)
 
-        move(0)
-        scatter(1, 0, S, y[1][:])
-        move(1)
-        back = []
-        for h in range(4):
-            bank = psum.tile([P, 2, P], F32, name=f"back{h}", tag=f"acc{h}")
-            for g in range(2):
-                nc.tensor.transpose(bank[:, g, :], turned[h][:, g, :].bitcast(F32), identity[:])
-            back.append(bank[:].rearrange("p g c -> p (g c)").bitcast(BF16).rearrange("p (c t) -> p c t", t=2))
-        STAGE = 2 * GROUP
-        for h in range(2):
-            nc.scalar.copy(out_bf[:, h * STAGE : (h + 1) * STAGE, 0:2], back[h])
-        nc.scalar.copy(out_bf[:, U - PARK :, 2:4], back[3][:, STAGE - PARK :])
-        nc.scalar.copy(out_bf[:, 2 * STAGE : 3 * STAGE, 0:2], back[2])
-        nc.scalar.copy(out_bf[:, U - PARK :, 0:2], out_bf[:, U - PARK :, 2:4])
-        nc.scalar.copy(out_bf[:, 3 * STAGE : U - PARK, 0:2], back[3][:, : STAGE - PARK])
-
-        scatter(2, 0, S, y[2][:])
-        nc.sync.dma_start(rows_of(out_rows, 2), win[2][:])
-        stages_bf = out_bf[:].rearrange("p (g c) t -> p g c t", c=STAGE)
-        stages = win[2][:].rearrange("p (g c) -> p g c", c=STAGE)
-        gp_round(stages_bf[:, :3, :PARK, 3], stages[:, :3, :PARK])
-        gp_round(stages_bf[:, :3, PARK:, 2], stages[:, :3, PARK:])
-        gp_round(stages_bf[:, :3, :PARK, 2], stages_bf[:, :3, :PARK, 3])
-        nc.scalar.copy(stages_bf[:, 3, :, 2], stages[:, 3])
-
-        scatter(3, 0, S, y[3][:])
-        nc.sync.dma_start(rows_of(out_rows, 3), win[3][:])
-        for a, b in ROUNDED:
-            copy = nc.vector.tensor_copy if a < VECTOR_COLS else nc.scalar.copy
-            copy(out_bf[:, a:b, 3], win[3][:, a:b])
+        nc.gpsimd.tensor_copy(*rounded(0, 0, U))
+        for a, b in PAIRED:
+            nc.gpsimd.tensor_copy(*rounded(1, a, b))
+        nc.vector.tensor_copy(*rounded(3, 0, VECTOR_COLS))
+        for a, b in VECTOR_TAIL:
+            nc.vector.tensor_copy(*rounded(2, a, b))
+        for a, b in SCALAR_TAIL:
+            for t in (2, 3):
+                nc.scalar.copy(*rounded(t, a, b))
+        for a, b in WOVEN_VECTOR:
+            nc.vector.tensor_copy(quad_words[:, a:b], woven[:, a:b])
+        for a, b in WOVEN_SCALAR:
+            nc.scalar.copy(quad_words[:, a:b], woven[:, a:b])
 
         stored = 0
         for a, b in QUANTISED:

@@ -24,13 +24,8 @@ HALF_N = N // 2
 QUADS = HALF_N // PACK
 LEAD = 256
 GATHERED = ((0, 128), (128, 256), (256, 512))
-VECTOR_COLS = 640
-PAIRED = ((0, 256), (256, 512), (512, 768), (768, 1024))
-VECTOR_TAIL = ((0, 256), (256, 640))
-SCALAR_TAIL = ((640, 832), (832, 1024))
-WOVEN_VECTOR = ((0, 256), (256, 512))
-WOVEN_SCALAR = ((640, 768), (512, 640), (768, 1024))
-QUANTISED = ((0, 256), (256, 512), (512, 768), (768, 1024))
+CHUNK = 256
+CHUNKS = U // CHUNK
 STORE_ENDS = (256, 768, 1024)
 
 
@@ -62,15 +57,14 @@ def tile_picked_kvput_none_po_kernel(
             nc.sync.dma_start(xs_all[r:P:QUADRANT, :].bitcast(I32), x_scales[0][r:SCALE_ROWS:PACK, :].bitcast(I32))
         nc.sync.dma_start(w_raw[1][:], w_rows[:, :, HALF_N:])
         nc.sync.dma_start(xw_all[:].bitcast(I32), x_words[0].rearrange("p c r -> p (c r)").bitcast(I32))
-        nc.sync.dma_start(win[0][:], mem_rows[:, 0, :])
         nc.sync.dma_start(slot_sb[:], slot)
-        for t in (1, 3, 2):
+        for t in (0, 1, 3, 2):
             nc.sync.dma_start(win[t][:], mem_rows[:, t, :])
 
         xs = keep.tile([P, S], U8, name="xs", align_bytes=64)
         nc.vector.tensor_copy(xs[:], xs_all[:].indirect(offs_sb[:]))
 
-        w_bf = [keep.tile([P, 2, P, PACK], BF16, name=f"w_bf{u}", tag=f"w_bf{u}", align_bytes=64) for u in range(2)]
+        w_bf = [keep.tile([P, 2, P, PACK], BF16, name=f"w_bf{u}", align_bytes=64) for u in range(2)]
 
         def w_share(h, u):
             src = w_raw[h][:].rearrange("p j (l t) -> p l t j", t=PACK)
@@ -93,7 +87,7 @@ def tile_picked_kvput_none_po_kernel(
         nc.gpsimd.tensor_copy(*w_share(1, 1))
         quantise_w(0)
         quantise_w(1)
-        xw = keep.tile([P, S], U32, name="xw", tag="w_bf0", align_bytes=64)
+        xw = keep.tile([P, S], U32, name="xw", align_bytes=64)
 
         def project(t, a, b, acc):
             nc.tensor.matmul_mx(
@@ -109,9 +103,11 @@ def tile_picked_kvput_none_po_kernel(
         def target(t, a, b):
             return win[t][:].indirect(slot_sb[:, a // STRIPE : b // STRIPE])
 
-        pair_words = keep.tile([P, 2 * U], F32, name="pair_words", align_bytes=64)
-        y = {t: keep.tile([P, S], F32, name=f"y{t}", align_bytes=64)[:] for t in range(2)}
-        y[3], y[2] = pair_words[:, U : U + S], pair_words[:, U + S :]
+        pairs = [keep.tile([P, 2 * CHUNK], F32, name=f"pairs{g}", align_bytes=64) for g in range(CHUNKS)]
+        y = {t: keep.tile([P, S], F32, name=f"y{t}", align_bytes=64)[:] for t in (0, 1, 3)}
+        halves = {(t, a): y[t][:, a : a + LEAD] for t in y for a in (0, LEAD)}
+        halves[2, 0] = keep.tile([P, LEAD], F32, name="y2", align_bytes=64)[:]
+        halves[2, LEAD] = pairs[CHUNKS - 1][:, CHUNK:]
         for a, b in GATHERED:
             nc.vector.tensor_copy(xw[:, a:b], xw_all[:].indirect(offs_sb[:, a // STRIPE : b // STRIPE]))
             if b <= LEAD:
@@ -128,57 +124,55 @@ def tile_picked_kvput_none_po_kernel(
             for i, (t, a) in enumerate(pieces):
                 project(t, a, a + LEAD, acc[:, i])
             for i, (t, a) in enumerate(pieces):
-                copy(y[t][:, a : a + LEAD], acc[:, i])
+                copy(halves[t, a], acc[:, i])
 
         nc.scalar.activation(target(0, 0, LEAD), y[0][:, :LEAD], COPY)
         through("acc0", nc.vector.tensor_copy, (1, 0))
         through("acc1", nc.vector.tensor_copy, (1, LEAD))
         through("acc2", nc.vector.tensor_copy, (3, 0))
         through("acc1", nc.scalar.copy, (0, LEAD), (3, LEAD))
-        through("acc2", nc.scalar.copy, (2, 0), (2, LEAD))
+        through("acc1", nc.scalar.copy, (2, 0), (2, LEAD))
         nc.vector.tensor_copy(target(1, 0, S), y[1])
         nc.scalar.activation(target(0, LEAD, S), y[0][:, LEAD:], COPY)
-        nc.scalar.activation(target(2, 0, LEAD), y[2][:, :LEAD], COPY)
-        nc.scalar.activation(target(2, LEAD, S), y[2][:, LEAD:], COPY)
+        nc.scalar.activation(target(2, 0, LEAD), halves[2, 0], COPY)
+        nc.scalar.activation(target(2, LEAD, S), halves[2, LEAD], COPY)
         nc.vector.tensor_copy(target(3, 0, S), y[3])
-        for t in (0, 1, 3, 2):
+        for t in (1, 0, 3, 2):
             nc.sync.dma_start(out_rows[:, t, :], win[t][:])
 
-        pairs = pair_words[:].bitcast(BF16).rearrange("p (u c e) -> p u c e", u=2, e=2)
-        out_bf = keep.tile([P, U, PACK], BF16, name="out_bf", align_bytes=64)
+        quads = [keep.tile([P, CHUNK, 2], F32, name=f"quads{g}", align_bytes=64) for g in range(CHUNKS)]
         codes = keep.tile([P, U], U32, name="codes", align_bytes=64)
         scales = keep.tile([P, U], U8, name="scales", align_bytes=64)
 
-        def rounded(t, a, b):
-            return pairs[:, t // 2, a:b, t % 2], win[t][:, a:b]
+        def rounded(t, g):
+            values = pairs[g][:].bitcast(BF16).rearrange("p (u c e) -> p u c e", u=2, e=2)
+            return values[:, t // 2, :, t % 2], win[t][:, g * CHUNK : (g + 1) * CHUNK]
 
-        woven = pair_words[:].rearrange("p (u c) -> p c u", u=2)
-        quad_words = out_bf[:].rearrange("p c t -> p (c t)").bitcast(F32).rearrange("p (c u) -> p c u", u=2)
+        def weave(copy, g):
+            copy(quads[g][:], pairs[g][:].rearrange("p (u c) -> p c u", u=2))
 
-        nc.gpsimd.tensor_copy(*rounded(0, 0, U))
-        for a, b in PAIRED:
-            nc.gpsimd.tensor_copy(*rounded(1, a, b))
-        nc.vector.tensor_copy(*rounded(3, 0, VECTOR_COLS))
-        for a, b in VECTOR_TAIL:
-            nc.vector.tensor_copy(*rounded(2, a, b))
-        for a, b in SCALAR_TAIL:
-            for t in (2, 3):
-                nc.scalar.copy(*rounded(t, a, b))
-        for a, b in WOVEN_VECTOR:
-            nc.vector.tensor_copy(quad_words[:, a:b], woven[:, a:b])
-        for a, b in WOVEN_SCALAR:
-            nc.scalar.copy(quad_words[:, a:b], woven[:, a:b])
-
-        stored = 0
-        for a, b in QUANTISED:
+        def quantise_out(g):
+            a, b = g * CHUNK, (g + 1) * CHUNK
             nc.vector.quantize_mx(
                 out=codes[:, a:b].bitcast(FP8X4),
                 scales=scales[:, a:b],
-                in_=out_bf[:, a:b, :].rearrange("p c t -> p (c t)"),
+                in_=quads[g][:].rearrange("p c u -> p (c u)").bitcast(BF16),
             )
             if b in STORE_ENDS:
-                nc.sync.dma_start(out_words[:, stored:b], codes[:, stored:b].bitcast(I32))
-                stored = b
+                begin = max([end for end in STORE_ENDS if end < b], default=0)
+                nc.sync.dma_start(out_words[:, begin:b], codes[:, begin:b].bitcast(I32))
+
+        for t in range(2):
+            for g in range(CHUNKS):
+                nc.gpsimd.tensor_copy(*rounded(t, g))
+        for t in (3, 2):
+            for g in range(CHUNKS - 1):
+                nc.vector.tensor_copy(*rounded(t, g))
+            nc.scalar.copy(*rounded(t, CHUNKS - 1))
+        for g in range(CHUNKS):
+            weave(nc.vector.tensor_copy if g < CHUNKS // 2 else nc.scalar.copy, g)
+        for g in range(CHUNKS):
+            quantise_out(g)
         for r in range(PACK):
             queue = nc.scalar if r % 2 == 0 else nc.sync
             queue.dma_start(out_2[0][r:SCALE_ROWS:PACK, :].bitcast(I32), scales[r:P:QUADRANT, :].bitcast(I32))

@@ -26,6 +26,7 @@ LEAD = 256
 GATHERED = ((0, 128), (128, 256), (256, 512))
 CHUNK = 256
 CHUNKS = U // CHUNK
+LAST = CHUNKS - 1
 STORE_ENDS = (256, 768, 1024)
 
 
@@ -106,8 +107,7 @@ def tile_picked_kvput_none_po_kernel(
         pairs = [keep.tile([P, 2 * CHUNK], F32, name=f"pairs{g}", align_bytes=64) for g in range(CHUNKS)]
         y = {t: keep.tile([P, S], F32, name=f"y{t}", align_bytes=64)[:] for t in (0, 1, 3)}
         halves = {(t, a): y[t][:, a : a + LEAD] for t in y for a in (0, LEAD)}
-        halves[2, 0] = keep.tile([P, LEAD], F32, name="y2", align_bytes=64)[:]
-        halves[2, LEAD] = pairs[CHUNKS - 1][:, CHUNK:]
+        halves[2, 0], halves[2, LEAD] = pairs[LAST][:, :CHUNK], pairs[LAST][:, CHUNK:]
         for a, b in GATHERED:
             nc.vector.tensor_copy(xw[:, a:b], xw_all[:].indirect(offs_sb[:, a // STRIPE : b // STRIPE]))
             if b <= LEAD:
@@ -163,12 +163,13 @@ def tile_picked_kvput_none_po_kernel(
                 nc.sync.dma_start(out_words[:, begin:b], codes[:, begin:b].bitcast(I32))
 
         for t in range(2):
-            for g in range(CHUNKS):
+            for g in range(LAST):
                 nc.gpsimd.tensor_copy(*rounded(t, g))
+            nc.vector.tensor_copy(*rounded(t, LAST))
         for t in (3, 2):
-            for g in range(CHUNKS - 1):
+            for g in range(LAST):
                 nc.vector.tensor_copy(*rounded(t, g))
-            nc.scalar.copy(*rounded(t, CHUNKS - 1))
+            nc.scalar.copy(*rounded(t, LAST))
         for g in range(CHUNKS):
             weave(nc.vector.tensor_copy if g < CHUNKS // 2 else nc.scalar.copy, g)
         for g in range(CHUNKS):

@@ -27,7 +27,9 @@ GATHERED = ((0, 128), (128, 256), (256, 512))
 CHUNK = 256
 CHUNKS = U // CHUNK
 LAST = CHUNKS - 1
-STORE_ENDS = (256, 768, 1024)
+QUANTISED = ((0, 256), (256, 512), (512, 768), (768, 896), (896, 1024))
+VECTOR_WOVEN = 512
+STORE_ENDS = (512, 896, 1024)
 
 
 def tile_picked_kvput_none_po_kernel(
@@ -140,7 +142,7 @@ def tile_picked_kvput_none_po_kernel(
         for t in (1, 0, 3, 2):
             nc.sync.dma_start(out_rows[:, t, :], win[t][:])
 
-        quads = [keep.tile([P, CHUNK, 2], F32, name=f"quads{g}", align_bytes=64) for g in range(CHUNKS)]
+        quads = {a: keep.tile([P, b - a, 2], F32, name=f"quads{a}", align_bytes=64) for a, b in QUANTISED}
         codes = keep.tile([P, U], U32, name="codes", align_bytes=64)
         scales = keep.tile([P, U], U8, name="scales", align_bytes=64)
 
@@ -148,15 +150,16 @@ def tile_picked_kvput_none_po_kernel(
             values = pairs[g][:].bitcast(BF16).rearrange("p (u c e) -> p u c e", u=2, e=2)
             return values[:, t // 2, :, t % 2], win[t][:, g * CHUNK : (g + 1) * CHUNK]
 
-        def weave(copy, g):
-            copy(quads[g][:], pairs[g][:].rearrange("p (u c) -> p c u", u=2))
+        def weave(a, b):
+            copy = nc.vector.tensor_copy if a < VECTOR_WOVEN else nc.scalar.copy
+            g, first = divmod(a, CHUNK)
+            copy(quads[a][:], pairs[g][:].rearrange("p (u c) -> p c u", u=2)[:, first : first + b - a])
 
-        def quantise_out(g):
-            a, b = g * CHUNK, (g + 1) * CHUNK
+        def quantise_out(a, b):
             nc.vector.quantize_mx(
                 out=codes[:, a:b].bitcast(FP8X4),
                 scales=scales[:, a:b],
-                in_=quads[g][:].rearrange("p c u -> p (c u)").bitcast(BF16),
+                in_=quads[a][:].rearrange("p c u -> p (c u)").bitcast(BF16),
             )
             if b in STORE_ENDS:
                 begin = max([end for end in STORE_ENDS if end < b], default=0)
@@ -170,10 +173,10 @@ def tile_picked_kvput_none_po_kernel(
             for g in range(LAST):
                 nc.vector.tensor_copy(*rounded(t, g))
             nc.scalar.copy(*rounded(t, LAST))
-        for g in range(CHUNKS):
-            weave(nc.vector.tensor_copy if g < CHUNKS // 2 else nc.scalar.copy, g)
-        for g in range(CHUNKS):
-            quantise_out(g)
+        for a, b in QUANTISED:
+            weave(a, b)
+        for a, b in QUANTISED:
+            quantise_out(a, b)
         for r in range(PACK):
             queue = nc.scalar if r % 2 == 0 else nc.sync
             queue.dma_start(out_2[0][r:SCALE_ROWS:PACK, :].bitcast(I32), scales[r:P:QUADRANT, :].bitcast(I32))

@@ -20,9 +20,9 @@ STRIPE = 16
 QUADRANT = 32
 SCALE_ROWS = 16
 
-HALF_N = N // 2
-QUADS = HALF_N // PACK
+VECTOR_QUADS = 96
 LEAD = 256
+BANK = 512
 GATHERED = ((0, 128), (128, 256), (256, 512))
 CHUNK = 256
 CHUNKS = U // CHUNK
@@ -49,16 +49,16 @@ def tile_picked_kvput_none_po_kernel(
         slot_sb = keep.tile([P, S // STRIPE], U16, name="slot_sb")
         xs_all = keep.tile([P, T], U8, name="xs_all", align_bytes=64)
         xw_all = keep.tile([P, T], U32, name="xw_all", tag="xw_all", align_bytes=64)
-        w_raw = [keep.tile([P, PACK, HALF_N], F32, name=f"w_raw{h}", align_bytes=64) for h in range(2)]
+        w_raw = [keep.tile([P, 2, N], F32, name=f"w_raw{h}", align_bytes=64) for h in range(2)]
         win = [keep.tile([P, U], F32, name=f"win{t}", align_bytes=64) for t in range(PACK)]
 
         nc.vector.memset(xs_all[:].bitcast(I32), 0)
 
         nc.sync.dma_start(offs_sb[:], offs)
-        nc.sync.dma_start(w_raw[0][:], w_rows[:, :, :HALF_N])
+        nc.sync.dma_start(w_raw[0][:], w_rows[:, :2, :])
         for r in range(PACK):
             nc.sync.dma_start(xs_all[r:P:QUADRANT, :].bitcast(I32), x_scales[0][r:SCALE_ROWS:PACK, :].bitcast(I32))
-        nc.sync.dma_start(w_raw[1][:], w_rows[:, :, HALF_N:])
+        nc.sync.dma_start(w_raw[1][:], w_rows[:, 2:, :])
         nc.sync.dma_start(xw_all[:].bitcast(I32), x_words[0].rearrange("p c r -> p (c r)").bitcast(I32))
         nc.sync.dma_start(slot_sb[:], slot)
         for t in (0, 1, 3, 2):
@@ -69,12 +69,12 @@ def tile_picked_kvput_none_po_kernel(
 
         w_bf = [keep.tile([P, 2, P, PACK], BF16, name=f"w_bf{u}", align_bytes=64) for u in range(2)]
 
-        def w_share(h, u):
+        def w_share(h, u, a=0, b=P):
             src = w_raw[h][:].rearrange("p j (l t) -> p l t j", t=PACK)
             dst = w_bf[u][:].rearrange("p e l j -> p l e j")
-            return dst[:, h * QUADS : (h + 1) * QUADS], src[:, :, 2 * u : 2 * u + 2]
+            return dst[:, a:b, :, 2 * h : 2 * h + 2], src[:, a:b, 2 * u : 2 * u + 2]
 
-        w_words = {t: keep.tile([P, P], U32, name=f"w_words{t}", align_bytes=64)[:] for t in range(2)}
+        w_words = {t: keep.tile([P, P], U32, name=f"w_words{t}", tag=f"w_words{t}", align_bytes=64)[:] for t in range(2)}
         w_scales = [keep.tile([P, P], U8, name=f"w_scales{t}", align_bytes=64) for t in range(PACK)]
 
         def quantise_w(t):
@@ -86,8 +86,9 @@ def tile_picked_kvput_none_po_kernel(
 
         nc.scalar.activation(*w_share(0, 0), COPY)
         nc.gpsimd.tensor_copy(*w_share(0, 1))
-        nc.scalar.copy(*w_share(1, 0))
-        nc.gpsimd.tensor_copy(*w_share(1, 1))
+        nc.vector.tensor_copy(*w_share(1, 0, 0, VECTOR_QUADS))
+        nc.scalar.copy(*w_share(1, 0, VECTOR_QUADS, P))
+        nc.scalar.copy(*w_share(1, 1))
         quantise_w(0)
         quantise_w(1)
         xw = keep.tile([P, S], U32, name="xw", align_bytes=64)
@@ -113,27 +114,27 @@ def tile_picked_kvput_none_po_kernel(
         for a, b in GATHERED:
             nc.vector.tensor_copy(xw[:, a:b], xw_all[:].indirect(offs_sb[:, a // STRIPE : b // STRIPE]))
             if b <= LEAD:
-                lead = psum.tile([P, b - a], F32, name=f"lead{a}", tag=f"lead{a}")
+                lead = psum.tile([P, b - a], F32, name=f"lead{a}", offset=a // P * BANK * 4)
                 project(0, a, b, lead[:])
                 nc.scalar.copy(y[0][:, a:b], lead[:])
-        late_words = keep.tile([P, 2 * P], U32, name="late_words", tag="xw_all", align_bytes=64)
-        w_words[2], w_words[3] = late_words[:, :P], late_words[:, P:]
+        w_words[3] = keep.tile([P, P], U32, name="w_words3", tag="xw_all", align_bytes=64)[:]
         quantise_w(3)
-        quantise_w(2)
 
-        def through(tag, copy, *pieces):
-            acc = psum.tile([P, len(pieces), LEAD], F32, name=f"acc{pieces[0][0]}_{pieces[0][1]}", tag=tag)
+        def through(copy, bank, banks, *pieces):
+            acc = psum.tile([P, banks * BANK], F32, name=f"acc{pieces[0][0]}_{pieces[0][1]}", offset=bank * BANK * 4)
             for i, (t, a) in enumerate(pieces):
-                project(t, a, a + LEAD, acc[:, i])
+                project(t, a, a + LEAD, acc[:, i * LEAD : (i + 1) * LEAD])
             for i, (t, a) in enumerate(pieces):
-                copy(halves[t, a], acc[:, i])
+                copy(halves[t, a], acc[:, i * LEAD : (i + 1) * LEAD])
 
         nc.scalar.activation(target(0, 0, LEAD), y[0][:, :LEAD], COPY)
-        through("acc0", nc.vector.tensor_copy, (1, 0))
-        through("acc1", nc.vector.tensor_copy, (1, LEAD))
-        through("acc2", nc.vector.tensor_copy, (3, 0))
-        through("acc1", nc.scalar.copy, (0, LEAD), (3, LEAD))
-        through("acc1", nc.scalar.copy, (2, 0), (2, LEAD))
+        through(nc.vector.tensor_copy, 2, 1, (1, 0))
+        through(nc.vector.tensor_copy, 3, 2, (1, LEAD))
+        w_words[2] = keep.tile([P, P], U32, name="w_words2", tag="w_words1", align_bytes=64)[:]
+        quantise_w(2)
+        through(nc.scalar.copy, 3, 1, (0, LEAD), (3, 0))
+        through(nc.scalar.copy, 4, 1, (3, LEAD))
+        through(nc.scalar.copy, 4, 1, (2, 0), (2, LEAD))
         nc.vector.tensor_copy(target(1, 0, S), y[1])
         nc.scalar.activation(target(0, LEAD, S), y[0][:, LEAD:], COPY)
         nc.scalar.activation(target(2, 0, LEAD), halves[2, 0], COPY)

@@ -54,8 +54,8 @@ def tile_picked_kvput_none_po_kernel(
 
         nc.vector.memset(xs_all[:].bitcast(I32), 0)
 
-        nc.sync.dma_start(offs_sb[:], offs)
         nc.sync.dma_start(w_raw[0][:], w_rows[:, :2, :])
+        nc.sync.dma_start(offs_sb[:], offs)
         for r in range(PACK):
             nc.sync.dma_start(xs_all[r:P:QUADRANT, :].bitcast(I32), x_scales[0][r:SCALE_ROWS:PACK, :].bitcast(I32))
         nc.sync.dma_start(w_raw[1][:], w_rows[:, 2:, :])
@@ -108,9 +108,9 @@ def tile_picked_kvput_none_po_kernel(
             return win[t][:].indirect(slot_sb[:, a // STRIPE : b // STRIPE])
 
         pairs = [keep.tile([P, 2 * CHUNK], F32, name=f"pairs{g}", align_bytes=64) for g in range(CHUNKS)]
-        y = {t: keep.tile([P, S], F32, name=f"y{t}", align_bytes=64)[:] for t in (0, 1, 3)}
+        y = {t: keep.tile([P, S], F32, name=f"y{t}", align_bytes=64)[:] for t in range(PACK)}
         halves = {(t, a): y[t][:, a : a + LEAD] for t in y for a in (0, LEAD)}
-        halves[2, 0], halves[2, LEAD] = pairs[LAST][:, :CHUNK], pairs[LAST][:, CHUNK:]
+        halves[2, 0] = pairs[LAST][:, CHUNK // 2 : CHUNK // 2 + LEAD]
         for a, b in GATHERED:
             nc.vector.tensor_copy(xw[:, a:b], xw_all[:].indirect(offs_sb[:, a // STRIPE : b // STRIPE]))
             if b <= LEAD:

@@ -22,6 +22,7 @@ SCALE_ROWS = 16
 
 VECTOR_QUADS = 96
 LEAD = 256
+LONG = 384
 BANK = 512
 GATHERED = ((0, 128), (128, 256), (256, 512))
 CHUNK = 256
@@ -110,7 +111,7 @@ def tile_picked_kvput_none_po_kernel(
         pairs = [keep.tile([P, 2 * CHUNK], F32, name=f"pairs{g}", align_bytes=64) for g in range(CHUNKS)]
         y = {t: keep.tile([P, S], F32, name=f"y{t}", align_bytes=64)[:] for t in range(PACK)}
         halves = {(t, a): y[t][:, a : a + LEAD] for t in y for a in (0, LEAD)}
-        halves[2, 0] = pairs[LAST][:, CHUNK // 2 : CHUNK // 2 + LEAD]
+        parked = pairs[LAST][:, CHUNK - LONG // 2 : CHUNK + LONG // 2]
         for a, b in GATHERED:
             nc.vector.tensor_copy(xw[:, a:b], xw_all[:].indirect(offs_sb[:, a // STRIPE : b // STRIPE]))
             if b <= LEAD:
@@ -134,11 +135,15 @@ def tile_picked_kvput_none_po_kernel(
         quantise_w(2)
         through(nc.scalar.copy, 3, 1, (0, LEAD), (3, 0))
         through(nc.scalar.copy, 4, 1, (3, LEAD))
-        through(nc.scalar.copy, 4, 1, (2, 0), (2, LEAD))
+        acc = psum.tile([P, BANK], F32, name="acc2", offset=4 * BANK * 4)
+        for a in (0, LEAD):
+            project(2, a, a + LEAD, acc[:, a : a + LEAD])
+        nc.scalar.copy(parked, acc[:, :LONG])
+        nc.scalar.copy(y[2][:, LONG:], acc[:, LONG:])
         nc.vector.tensor_copy(target(1, 0, S), y[1])
         nc.scalar.activation(target(0, LEAD, S), y[0][:, LEAD:], COPY)
-        nc.scalar.activation(target(2, 0, LEAD), halves[2, 0], COPY)
-        nc.scalar.activation(target(2, LEAD, S), halves[2, LEAD], COPY)
+        nc.scalar.activation(target(2, 0, LONG), parked, COPY)
+        nc.scalar.activation(target(2, LONG, S), y[2][:, LONG:], COPY)
         nc.vector.tensor_copy(target(3, 0, S), y[3])
         for t in (1, 0, 3, 2):
             nc.sync.dma_start(out_rows[:, t, :], win[t][:])

@@ -22,12 +22,13 @@ SCALE_ROWS = 16
 
 VECTOR_QUADS = 96
 LEAD = 256
-LONG = 384
+LONG = 288
 BANK = 512
 GATHERED = ((0, 128), (128, 256), (256, 512))
 CHUNK = 256
 CHUNKS = U // CHUNK
 LAST = CHUNKS - 1
+PARKED = 2 * LAST * CHUNK - (LONG - CHUNK) // 2
 QUANTISED = ((0, 256), (256, 512), (512, 768), (768, 896), (896, 1024))
 VECTOR_WOVEN = 512
 STORE_ENDS = (512, 896, 1024)
@@ -108,18 +109,21 @@ def tile_picked_kvput_none_po_kernel(
         def target(t, a, b):
             return win[t][:].indirect(slot_sb[:, a // STRIPE : b // STRIPE])
 
-        pairs = [keep.tile([P, 2 * CHUNK], F32, name=f"pairs{g}", align_bytes=64) for g in range(CHUNKS)]
+        shelf = keep.tile([P, 2 * U], F32, name="pairs", align_bytes=64)
+        pairs = [shelf[:, 2 * g * CHUNK : 2 * (g + 1) * CHUNK] for g in range(CHUNKS)]
         y = {t: keep.tile([P, S], F32, name=f"y{t}", align_bytes=64)[:] for t in range(PACK)}
         halves = {(t, a): y[t][:, a : a + LEAD] for t in y for a in (0, LEAD)}
-        parked = pairs[LAST][:, CHUNK - LONG // 2 : CHUNK + LONG // 2]
+        parked = shelf[:, PARKED : PARKED + LONG]
         for a, b in GATHERED:
             nc.vector.tensor_copy(xw[:, a:b], xw_all[:].indirect(offs_sb[:, a // STRIPE : b // STRIPE]))
             if b <= LEAD:
                 lead = psum.tile([P, b - a], F32, name=f"lead{a}", offset=a // P * BANK * 4)
                 project(0, a, b, lead[:])
                 nc.scalar.copy(y[0][:, a:b], lead[:])
-        w_words[3] = keep.tile([P, P], U32, name="w_words3", tag="xw_all", align_bytes=64)[:]
+        late_words = keep.tile([P, 2 * P], U32, name="late_words", tag="xw_all", align_bytes=64)
+        w_words[3], w_words[2] = late_words[:, :P], late_words[:, P:]
         quantise_w(3)
+        quantise_w(2)
 
         def through(copy, bank, banks, *pieces):
             acc = psum.tile([P, banks * BANK], F32, name=f"acc{pieces[0][0]}_{pieces[0][1]}", offset=bank * BANK * 4)
@@ -128,14 +132,13 @@ def tile_picked_kvput_none_po_kernel(
             for i, (t, a) in enumerate(pieces):
                 copy(halves[t, a], acc[:, i * LEAD : (i + 1) * LEAD])
 
+        through(nc.scalar.copy, 2, 1, (1, 0))
         nc.scalar.activation(target(0, 0, LEAD), y[0][:, :LEAD], COPY)
-        through(nc.vector.tensor_copy, 2, 1, (1, 0))
-        through(nc.vector.tensor_copy, 3, 2, (1, LEAD))
-        w_words[2] = keep.tile([P, P], U32, name="w_words2", tag="w_words1", align_bytes=64)[:]
-        quantise_w(2)
-        through(nc.scalar.copy, 3, 1, (0, LEAD), (3, 0))
-        through(nc.scalar.copy, 4, 1, (3, LEAD))
-        acc = psum.tile([P, BANK], F32, name="acc2", offset=4 * BANK * 4)
+        through(nc.vector.tensor_copy, 3, 1, (1, LEAD))
+        through(nc.vector.tensor_copy, 4, 2, (0, LEAD))
+        through(nc.scalar.copy, 4, 1, (3, 0))
+        through(nc.scalar.copy, 5, 1, (3, LEAD))
+        acc = psum.tile([P, BANK], F32, name="acc2", offset=5 * BANK * 4)
         for a in (0, LEAD):
             project(2, a, a + LEAD, acc[:, a : a + LEAD])
         nc.scalar.copy(parked, acc[:, :LONG])
@@ -153,13 +156,13 @@ def tile_picked_kvput_none_po_kernel(
         scales = keep.tile([P, U], U8, name="scales", align_bytes=64)
 
         def rounded(t, g):
-            values = pairs[g][:].bitcast(BF16).rearrange("p (u c e) -> p u c e", u=2, e=2)
+            values = pairs[g].bitcast(BF16).rearrange("p (u c e) -> p u c e", u=2, e=2)
             return values[:, t // 2, :, t % 2], win[t][:, g * CHUNK : (g + 1) * CHUNK]
 
         def weave(a, b):
             copy = nc.vector.tensor_copy if a < VECTOR_WOVEN else nc.scalar.copy
             g, first = divmod(a, CHUNK)
-            copy(quads[a][:], pairs[g][:].rearrange("p (u c) -> p c u", u=2)[:, first : first + b - a])
+            copy(quads[a][:], pairs[g].rearrange("p (u c) -> p c u", u=2)[:, first : first + b - a])
 
         def quantise_out(a, b):
             nc.vector.quantize_mx(
@@ -175,9 +178,11 @@ def tile_picked_kvput_none_po_kernel(
             for g in range(LAST):
                 nc.gpsimd.tensor_copy(*rounded(t, g))
             nc.vector.tensor_copy(*rounded(t, LAST))
+        values = shelf[:].bitcast(BF16).rearrange("p (g u h c e) -> p h g u c e", u=2, h=2, g=CHUNKS, e=2)
+        nc.vector.tensor_copy(values[:, :, :LAST, 1, :, 1], win[3][:].rearrange("p (g h c) -> p h g c", h=2, g=CHUNKS)[:, :, :LAST])
+        for g in range(LAST):
+            nc.vector.tensor_copy(*rounded(2, g))
         for t in (3, 2):
-            for g in range(LAST):
-                nc.vector.tensor_copy(*rounded(t, g))
             nc.scalar.copy(*rounded(t, LAST))
         for a, b in QUANTISED:
             weave(a, b)

@@ -174,12 +174,15 @@ def tile_picked_kvput_none_po_kernel(
                 begin = max([end for end in STORE_ENDS if end < b], default=0)
                 nc.sync.dma_start(out_words[:, begin:b], codes[:, begin:b].bitcast(I32))
 
+        def rounded_low(t, parts):
+            values = shelf[:].bitcast(BF16).rearrange("p (g u h c e) -> p h g u c e", u=2, h=parts, g=CHUNKS, e=2)
+            source = win[t][:].rearrange("p (g h c) -> p h g c", h=parts, g=CHUNKS)
+            return values[:, :, :LAST, t // 2, :, t % 2], source[:, :, :LAST]
+
         for t in range(2):
-            for g in range(LAST):
-                nc.gpsimd.tensor_copy(*rounded(t, g))
+            nc.gpsimd.tensor_copy(*rounded_low(t, 1))
             nc.vector.tensor_copy(*rounded(t, LAST))
-        values = shelf[:].bitcast(BF16).rearrange("p (g u h c e) -> p h g u c e", u=2, h=2, g=CHUNKS, e=2)
-        nc.vector.tensor_copy(values[:, :, :LAST, 1, :, 1], win[3][:].rearrange("p (g h c) -> p h g c", h=2, g=CHUNKS)[:, :, :LAST])
+        nc.vector.tensor_copy(*rounded_low(3, 2))
         for g in range(LAST):
             nc.vector.tensor_copy(*rounded(2, g))
         for t in (3, 2):

from contextlib import ExitStack

import concourse.mybir as mybir

K, T, S, N, U = 512, 1024, 512, 512, 1024
FLOPS = 2 * K * N * S

F32 = mybir.dt.float32
BF16 = mybir.dt.bfloat16
I32 = mybir.dt.int32
U32 = mybir.dt.uint32
U16 = mybir.dt.uint16
U8 = mybir.dt.uint8
FP8X4 = mybir.dt.float8_e4m3fn_x4
COPY = mybir.ActivationFunctionType.Copy

P = 128
PACK = 4
STRIPE = 16
QUADRANT = 32
SCALE_ROWS = 16

VECTOR_QUADS = 96
LEAD = 256
LONG = 288
BANK = 512
GATHERED = ((0, 128), (128, 256), (256, 512))
CHUNK = 256
CHUNKS = U // CHUNK
LAST = CHUNKS - 1
PARKED = 2 * LAST * CHUNK - (LONG - CHUNK) // 2
QUANTISED = ((0, 256), (256, 512), (512, 768), (768, 896), (896, 1024))
VECTOR_WOVEN = 512
STORE_ENDS = (512, 896, 1024)


def tile_picked_kvput_none_po_kernel(
    tc, x_words, x_scales, mem, w1, offs, slot, out_0, out_1, out_2
):
    nc = tc.nc
    mem_rows = mem.rearrange("(p t) c -> p t c", t=PACK)
    out_rows = out_0.rearrange("(p t) c -> p t c", t=PACK)
    w_rows = w1.rearrange("(p j) n -> p j n", j=PACK)
    out_words = out_1[0].rearrange("p c r -> p (c r)").bitcast(I32)

    with ExitStack() as ctx:
        keep = ctx.enter_context(tc.tile_pool(name="keep", bufs=1))
        psum = ctx.enter_context(tc.psum_pool(name="psum", bufs=1))

        offs_sb = keep.tile([P, S // STRIPE], U16, name="offs_sb")
        slot_sb = keep.tile([P, S // STRIPE], U16, name="slot_sb")
        xs_all = keep.tile([P, T], U8, name="xs_all", align_bytes=64)
        xw_all = keep.tile([P, T], U32, name="xw_all", tag="xw_all", align_bytes=64)
        w_raw = [keep.tile([P, 2, N], F32, name=f"w_raw{h}", align_bytes=64) for h in range(2)]
        win = [keep.tile([P, U], F32, name=f"win{t}", align_bytes=64) for t in range(PACK)]

        nc.vector.memset(xs_all[:].bitcast(I32), 0)

        nc.sync.dma_start(w_raw[0][:], w_rows[:, :2, :])
        nc.sync.dma_start(offs_sb[:], offs)
        for r in range(PACK):
            nc.sync.dma_start(xs_all[r:P:QUADRANT, :].bitcast(I32), x_scales[0][r:SCALE_ROWS:PACK, :].bitcast(I32))
        nc.sync.dma_start(w_raw[1][:], w_rows[:, 2:, :])
        nc.sync.dma_start(xw_all[:].bitcast(I32), x_words[0].rearrange("p c r -> p (c r)").bitcast(I32))
        nc.sync.dma_start(slot_sb[:], slot)
        for t in (0, 1, 3, 2):
            nc.sync.dma_start(win[t][:], mem_rows[:, t, :])

        xs = keep.tile([P, S], U8, name="xs", align_bytes=64)
        nc.vector.tensor_copy(xs[:], xs_all[:].indirect(offs_sb[:]))

        w_bf = [keep.tile([P, 2, P, PACK], BF16, name=f"w_bf{u}", align_bytes=64) for u in range(2)]

        def w_share(h, u, a=0, b=P):
            src = w_raw[h][:].rearrange("p j (l t) -> p l t j", t=PACK)
            dst = w_bf[u][:].rearrange("p e l j -> p l e j")
            return dst[:, a:b, :, 2 * h : 2 * h + 2], src[:, a:b, 2 * u : 2 * u + 2]

        w_words = {t: keep.tile([P, P], U32, name=f"w_words{t}", tag=f"w_words{t}", align_bytes=64)[:] for t in range(2)}
        w_scales = [keep.tile([P, P], U8, name=f"w_scales{t}", align_bytes=64) for t in range(PACK)]

        def quantise_w(t):
            nc.vector.quantize_mx(
                out=w_words[t].bitcast(FP8X4),
                scales=w_scales[t][:],
                in_=w_bf[t // 2][:, t % 2].rearrange("p l j -> p (l j)"),
            )

        nc.scalar.activation(*w_share(0, 0), COPY)
        nc.gpsimd.tensor_copy(*w_share(0, 1))
        nc.vector.tensor_copy(*w_share(1, 0, 0, VECTOR_QUADS))
        nc.scalar.copy(*w_share(1, 0, VECTOR_QUADS, P))
        nc.scalar.copy(*w_share(1, 1))
        quantise_w(0)
        quantise_w(1)
        xw = keep.tile([P, S], U32, name="xw", align_bytes=64)

        def project(t, a, b, acc):
            nc.tensor.matmul_mx(
                out=acc,
                lhsT=w_words[t].bitcast(FP8X4),
                lhsT_scale=w_scales[t][:],
                rhs=xw[:, a:b].bitcast(FP8X4),
                rhs_scale=xs[:, a:b],
                start=True,
                stop=True,
            )

        def target(t, a, b):
            return win[t][:].indirect(slot_sb[:, a // STRIPE : b // STRIPE])

        shelf = keep.tile([P, 2 * U], F32, name="pairs", align_bytes=64)
        pairs = [shelf[:, 2 * g * CHUNK : 2 * (g + 1) * CHUNK] for g in range(CHUNKS)]
        y = {t: keep.tile([P, S], F32, name=f"y{t}", align_bytes=64)[:] for t in range(PACK)}
        halves = {(t, a): y[t][:, a : a + LEAD] for t in y for a in (0, LEAD)}
        parked = shelf[:, PARKED : PARKED + LONG]
        for a, b in GATHERED:
            nc.vector.tensor_copy(xw[:, a:b], xw_all[:].indirect(offs_sb[:, a // STRIPE : b // STRIPE]))
            if b <= LEAD:
                lead = psum.tile([P, b - a], F32, name=f"lead{a}", offset=a // P * BANK * 4)
                project(0, a, b, lead[:])
                nc.scalar.copy(y[0][:, a:b], lead[:])
        late_words = keep.tile([P, 2 * P], U32, name="late_words", tag="xw_all", align_bytes=64)
        w_words[3], w_words[2] = late_words[:, :P], late_words[:, P:]
        quantise_w(3)
        quantise_w(2)

        def through(copy, bank, banks, *pieces):
            acc = psum.tile([P, banks * BANK], F32, name=f"acc{pieces[0][0]}_{pieces[0][1]}", offset=bank * BANK * 4)
            for i, (t, a) in enumerate(pieces):
                project(t, a, a + LEAD, acc[:, i * LEAD : (i + 1) * LEAD])
            for i, (t, a) in enumerate(pieces):
                copy(halves[t, a], acc[:, i * LEAD : (i + 1) * LEAD])

        through(nc.scalar.copy, 2, 1, (1, 0))
        nc.scalar.activation(target(0, 0, LEAD), y[0][:, :LEAD], COPY)
        through(nc.vector.tensor_copy, 3, 1, (1, LEAD))
        through(nc.vector.tensor_copy, 4, 2, (0, LEAD))
        through(nc.scalar.copy, 4, 1, (3, 0))
        through(nc.scalar.copy, 5, 1, (3, LEAD))
        acc = psum.tile([P, BANK], F32, name="acc2", offset=5 * BANK * 4)
        for a in (0, LEAD):
            project(2, a, a + LEAD, acc[:, a : a + LEAD])
        nc.scalar.copy(parked, acc[:, :LONG])
        nc.scalar.copy(y[2][:, LONG:], acc[:, LONG:])
        nc.vector.tensor_copy(target(1, 0, S), y[1])
        nc.scalar.activation(target(0, LEAD, S), y[0][:, LEAD:], COPY)
        nc.scalar.activation(target(2, 0, LONG), parked, COPY)
        nc.scalar.activation(target(2, LONG, S), y[2][:, LONG:], COPY)
        nc.vector.tensor_copy(target(3, 0, S), y[3])
        for t in (1, 0, 3, 2):
            nc.sync.dma_start(out_rows[:, t, :], win[t][:])

        quads = {a: keep.tile([P, b - a, 2], F32, name=f"quads{a}", align_bytes=64) for a, b in QUANTISED}
        codes = keep.tile([P, U], U32, name="codes", align_bytes=64)
        scales = keep.tile([P, U], U8, name="scales", align_bytes=64)

        def rounded(t, g):
            values = pairs[g].bitcast(BF16).rearrange("p (u c e) -> p u c e", u=2, e=2)
            return values[:, t // 2, :, t % 2], win[t][:, g * CHUNK : (g + 1) * CHUNK]

        def weave(a, b):
            copy = nc.vector.tensor_copy if a < VECTOR_WOVEN else nc.scalar.copy
            g, first = divmod(a, CHUNK)
            copy(quads[a][:], pairs[g].rearrange("p (u c) -> p c u", u=2)[:, first : first + b - a])

        def quantise_out(a, b):
            nc.vector.quantize_mx(
                out=codes[:, a:b].bitcast(FP8X4),
                scales=scales[:, a:b],
                in_=quads[a][:].rearrange("p c u -> p (c u)").bitcast(BF16),
            )
            if b in STORE_ENDS:
                begin = max([end for end in STORE_ENDS if end < b], default=0)
                nc.sync.dma_start(out_words[:, begin:b], codes[:, begin:b].bitcast(I32))

        def rounded_low(t, parts):
            values = shelf[:].bitcast(BF16).rearrange("p (g u h c e) -> p h g u c e", u=2, h=parts, g=CHUNKS, e=2)
            source = win[t][:].rearrange("p (g h c) -> p h g c", h=parts, g=CHUNKS)
            return values[:, :, :LAST, t // 2, :, t % 2], source[:, :, :LAST]

        for t in range(2):
            nc.gpsimd.tensor_copy(*rounded_low(t, 1))
            nc.vector.tensor_copy(*rounded(t, LAST))
        nc.vector.tensor_copy(*rounded_low(3, 2))
        for g in range(LAST):
            nc.vector.tensor_copy(*rounded(2, g))
        for t in (3, 2):
            nc.scalar.copy(*rounded(t, LAST))
        for a, b in QUANTISED:
            weave(a, b)
        for a, b in QUANTISED:
            quantise_out(a, b)
        for r in range(PACK):
            queue = nc.scalar if r % 2 == 0 else nc.sync
            queue.dma_start(out_2[0][r:SCALE_ROWS:PACK, :].bitcast(I32), scales[r:P:QUADRANT, :].bitcast(I32))
